import numpy as np
import ml_dtypes


def mxq(x, axis, fmt="e4m3"):
    dtype, down = {"e4m3": (ml_dtypes.float8_e4m3fn, 7), "e5m2": (ml_dtypes.float8_e5m2, 14)}[fmt]
    v = np.moveaxis(np.asarray(x, np.float32).astype(ml_dtypes.bfloat16).astype(np.float64), axis, -1)
    blocks = v.reshape(v.shape[:-1] + (-1, 32))
    amax = np.abs(blocks).max(-1, keepdims=True)
    byte = np.maximum(np.where(amax > 0, np.frexp(amax)[1] - 1 + 127, 0) - down, 1)
    scale = np.exp2(byte - 127.0)
    codes = (blocks / scale).astype(np.float32).astype(dtype).astype(np.float64)
    return np.moveaxis((codes * scale).reshape(v.shape), -1, axis)


WIDE = False


def mx_kscale(k):
    if not WIDE:
        return np.ones(k)
    levels = np.array([10, -10, 5, -5, 0])
    if k % 512:
        return np.exp2(np.random.permutation(np.resize(levels, k // 32))).repeat(32)
    a = np.empty((k // 512, 16))
    for p in range(k // 512):
        a[p, :8] = np.random.permutation(np.resize(levels, 8))
        for g in range(8):
            far = levels[np.abs(levels - a[p, g]) >= 10]
            a[p, g + 8] = far[np.random.randint(len(far))]
    return np.exp2(a.ravel()).repeat(32)


def f64(x):
    return np.asarray(x).astype(np.float64)


def striped(idx):
    return np.tile(np.asarray(idx).reshape(-1, 16).T, (8, 1)).astype(np.uint16)


def unstriped(offs):
    return offs[:16].T.reshape(-1).astype(np.int64)


E2M1 = np.array([0.0, 0.5, 1.0, 1.5, 2.0, 3.0, 4.0, 6.0, -0.0, -0.5, -1.0, -1.5, -2.0, -3.0, -4.0, -6.0])


def pack_weight(w, fmt):
    k, n = w.shape
    w = f64(np.asarray(w, np.float32).astype(ml_dtypes.bfloat16)).reshape(k // 32, 32, n)
    amax = np.abs(w).max(1)
    if fmt == "e4m3":
        byte = np.frexp(amax)[1] - 1 + 127 - 7
    else:
        mant, ex = np.frexp(amax / 6.0)
        byte = np.where(mant > 0.5, ex, ex - 1) + 127
    byte = np.clip(np.where(amax > 0, byte, 1), 1, 254)
    scaled = (w * np.exp2(127.0 - byte)[:, None, :]).reshape(k, n).astype(np.float32)
    by_word = np.ascontiguousarray(scaled.reshape(k // 512, 128, 4, n).transpose(0, 1, 3, 2))
    if fmt == "e4m3":
        words = by_word.astype(ml_dtypes.float8_e4m3fn).view(np.uint8)
    else:
        c = by_word.astype(ml_dtypes.float4_e2m1fn).view(np.uint8) & 0xF
        words = (c[..., 0::2] | (c[..., 1::2] << 4)).reshape(k // 512, 128, 2 * n)
    return np.ascontiguousarray(words), np.ascontiguousarray(byte.astype(np.uint8).reshape(k // 512, 16, n))


def unpack_weight(words, scales, fmt):
    g, _, n = scales.shape
    words = np.ascontiguousarray(words).reshape(g, 128, n, -1)
    if fmt == "e4m3":
        vals = words.view(ml_dtypes.float8_e4m3fn).astype(np.float64)
    else:
        nib = np.empty((g, 128, n, 4), np.uint8)
        nib[..., 0::2] = words & 0xF
        nib[..., 1::2] = words >> 4
        vals = E2M1[nib]
    vals = vals * np.repeat(np.exp2(scales.astype(np.float64) - 127.0), 8, axis=1)[..., None]
    return vals.transpose(0, 1, 3, 2).reshape(g * 512, n)


B, N, T, D, DV, NQ = 1, 512, 2048, 512, 256, 128


def setup_inputs():
    n = np.random.standard_normal
    idx = np.random.permutation(T)[:B * N]
    s = mx_kscale(D)[:, None]
    u = np.ones(T)
    u[idx] = mx_kscale(B * N)
    r = np.random.uniform(0.5, 2.0, T)
    k = n((D, T)) / s
    v = n((DV, T)) / (u * r)
    kp = pack_weight(k, "e4m3")
    return {
        "qT": (n((B, D, NQ)) * s * (0.60 / np.sqrt(D))).astype(np.float32),
        "k_words": kp[0],
        "k_scales": kp[1],
        "vT": v.astype(np.float32),
        "vs": np.tile(u * r, (128, 1)).astype(np.float32),
        "offs": striped(idx),
    }


def reference(qT, k_words, k_scales, vT, vs, offs):
    idx = unstriped(offs)
    k = unpack_weight(k_words, k_scales, "e4m3")
    v = f64(vT)
    pick = lambda x: x[:, idx].reshape(x.shape[0], B, N).transpose(1, 0, 2)
    q = f64(qT)
    score = mxq(q, 1, "e4m3").transpose(0, 2, 1) @ pick(k)
    m = score.max(-1, keepdims=True)
    p = np.exp(score - m)
    total = p.sum(-1, keepdims=True)
    w = p * pick(f64(vs))[:, :1, :]
    y = mxq(w, 2, "e4m3") @ mxq(pick(v).transpose(0, 2, 1), 1, "e4m3")
    y = y / total
    return y

@@ -1,0 +1,131 @@
+from contextlib import ExitStack
+
+import concourse.mybir as mybir
+from concourse.masks import make_identity
+
+N, T, D, DV, NQ = 512, 2048, 512, 256, 128
+FLOPS = 2 * NQ * N * (D + DV)
+
+F32 = mybir.dt.float32
+BF16 = mybir.dt.bfloat16
+I32 = mybir.dt.int32
+U32 = mybir.dt.uint32
+U16 = mybir.dt.uint16
+U8 = mybir.dt.uint8
+FP8X4 = mybir.dt.float8_e4m3fn_x4
+ACT = mybir.ActivationFunctionType
+ALU = mybir.AluOpType
+
+P = 128
+PACK = 4
+VS_ROW = P - 1
+
+
+def tile_attend_soft_topk_kernel(tc, qT, k_words, k_scales, vT, vs, offs, out):
+    nc = tc.nc
+    with ExitStack() as ctx:
+        sb = ctx.enter_context(tc.tile_pool(name="sb", bufs=1))
+        ps = ctx.enter_context(tc.psum_pool(name="ps", bufs=1))
+
+        offsets = sb.tile([P, N // 16], U16, name="offsets")
+        q_raw = sb.tile([P, PACK, NQ], F32, name="q_raw")
+        key_pool = sb.tile([P, T], I32, name="key_pool", tag="slot_k", align_bytes=64)
+        key_scale_pool = sb.tile([P, T // 4], I32, name="key_scale_pool", tag="slot_s", align_bytes=64)
+        vs_pool = sb.tile([P, T], F32, name="vs_pool", tag="slot_v")
+        v_pool0 = sb.tile([P, T], F32, name="v_pool0")
+
+        nc.vector.memset(key_scale_pool[:], 0)
+        nc.vector.memset(vs_pool[:VS_ROW, :], 0.0)
+        nc.sync.dma_start(offsets[:], offs)
+        nc.sync.dma_start(vs_pool[VS_ROW:, :], vs[0:1, :])
+        for quad in range(4):
+            nc.scalar.dma_start(key_scale_pool[32 * quad : 32 * quad + 4, :], k_scales[0, 4 * quad : 4 * quad + 4, :].bitcast(I32))
+        nc.sync.dma_start(q_raw[:], qT[0].rearrange("(p t) q -> p t q", t=PACK))
+        nc.sync.dma_start(key_pool[:], k_words[0].rearrange("p t r -> p (t r)").bitcast(I32))
+        nc.sync.dma_start(v_pool0[:], vT[:P, :])
+
+        ident = sb.tile([P, P], F32, name="ident")
+        make_identity(nc, ident[:])
+
+        key_scales = sb.tile([P, N], U8, name="key_scales", align_bytes=64)
+        nc.vector.tensor_copy(key_scales[:], key_scale_pool[:].bitcast(U8).indirect(offsets[:]))
+
+        q_bf = sb.tile([P, NQ, PACK], BF16, name="q_bf", align_bytes=64)
+        nc.scalar.copy(q_bf[:], q_raw[:].rearrange("p t q -> p q t"))
+
+        vs_row = sb.tile([P, N], F32, name="vs_row")
+        nc.vector.tensor_copy(vs_row[:], vs_pool[:].indirect(offsets[:]))
+
+        v_pool1 = sb.tile([P, T], F32, name="v_pool1", tag="slot_v")
+        nc.sync.dma_start(v_pool1[:], vT[P:, :])
+
+        q_codes = sb.tile([P, NQ], U32, name="q_codes", align_bytes=64)
+        q_scales = sb.tile([P, NQ], U8, name="q_scales", align_bytes=64)
+        nc.vector.quantize_mx(out=q_codes[:].bitcast(FP8X4), scales=q_scales[:], in_=q_bf[:].rearrange("p q t -> p (q t)"))
+
+        key_codes = sb.tile([P, N], U32, name="key_codes", tag="slot_s", align_bytes=64)
+        nc.vector.tensor_copy(key_codes[:], key_pool[:].bitcast(U32).indirect(offsets[:]))
+
+        vs_turned = ps.tile([P, PACK, P], F32, name="vs_turned")
+        for t in range(PACK):
+            nc.tensor.transpose(vs_turned[:, t, :], vs_row[:, t:N:PACK], ident[:])
+        vs_slot = sb.tile([P, PACK], F32, name="vs_slot")
+        nc.scalar.copy(vs_slot[:], vs_turned[:, :, VS_ROW])
+
+        scores = ps.tile([P, N], F32, name="scores")
+        nc.tensor.matmul_mx(out=scores[:], lhsT=q_codes[:].bitcast(FP8X4), lhsT_scale=q_scales[:],
+                            rhs=key_codes[:].bitcast(FP8X4), rhs_scale=key_scales[:], start=True, stop=True)
+        neg_max = sb.tile([P, 1], F32, name="neg_max")
+        nc.vector.tensor_reduce(neg_max[:], scores[:], mybir.AxisListType.X, ALU.max, negate=True)
+
+        def gather_values(v_pool, name, tag):
+            pairs = sb.tile([P, 2, P, 2], BF16, name=name, tag=tag, align_bytes=64)
+            nc.vector.tensor_copy(pairs[:].rearrange("f u p e -> f p u e"), v_pool[:].indirect(offsets[:]))
+            return pairs
+
+        def turn_values(h, pairs):
+            turned = ps.tile([P, 2, P], F32, name="v_turned%d" % h)
+            for u in range(2):
+                nc.tensor.transpose(turned[:, u, :], pairs[:, u].rearrange("f p e -> f (p e)").bitcast(F32), ident[:])
+            grouped = sb.tile([P, P, 2], F32, name="v_grouped%d" % h, align_bytes=64)
+            nc.scalar.copy(grouped[:], turned[:].rearrange("p u f -> p f u"))
+            return grouped
+
+        def quantize_values(h, grouped):
+            codes = sb.tile([P, P], U32, name="v_codes%d" % h, align_bytes=64)
+            scales = sb.tile([P, P], U8, name="v_scales%d" % h, align_bytes=64)
+            nc.vector.quantize_mx(out=codes[:].bitcast(FP8X4), scales=scales[:],
+                                  in_=grouped[:].rearrange("p f u -> p (f u)").bitcast(BF16))
+            return codes, scales
+
+        pairs0 = gather_values(v_pool0, "v_pairs0", "slot_k")
+
+        p_exp = sb.tile([P, PACK, P], F32, name="p_exp")
+        row_sum = sb.tile([P, 1], F32, name="row_sum")
+        nc.scalar.activation(p_exp[:], scores[:].rearrange("q (p t) -> q t p", t=PACK), ACT.Exp, bias=neg_max[:], accum_out=row_sum[:])
+        p_turned = ps.tile([P, PACK, NQ], F32, name="p_turned")
+        for t in range(PACK):
+            nc.tensor.transpose(p_turned[:, t, :], p_exp[:, t, :], ident[:])
+        grouped0 = turn_values(0, pairs0)
+
+        pairs1 = gather_values(v_pool1, "v_pairs1", "v_pairs1")
+        grouped1 = turn_values(1, pairs1)
+
+        w_bf = sb.tile([P, NQ, PACK], BF16, name="w_bf", align_bytes=64)
+        nc.vector.tensor_tensor(w_bf[:], p_turned[:].rearrange("p t q -> p q t"),
+                                vs_slot[:].unsqueeze(1).to_broadcast([P, NQ, PACK]), ALU.mult)
+        v0 = quantize_values(0, grouped0)
+        w_codes = sb.tile([P, NQ], U32, name="w_codes", align_bytes=64)
+        w_scales = sb.tile([P, NQ], U8, name="w_scales", align_bytes=64)
+        nc.vector.quantize_mx(out=w_codes[:].bitcast(FP8X4), scales=w_scales[:], in_=w_bf[:].rearrange("p q t -> p (q t)"))
+        inv_sum = sb.tile([P, 1], F32, name="inv_sum")
+        nc.vector.reciprocal(inv_sum[:], row_sum[:])
+        v1 = quantize_values(1, grouped1)
+
+        for h, (codes, scales) in enumerate((v0, v1)):
+            acc = ps.tile([NQ, P], F32, name="acc%d" % h)
+            nc.tensor.matmul_mx(out=acc[:], lhsT=w_codes[:].bitcast(FP8X4), lhsT_scale=w_scales[:],
+                                rhs=codes[:].bitcast(FP8X4), rhs_scale=scales[:], start=True, stop=True)
+            y = sb.tile([NQ, P], F32, name="y%d" % h)
+            nc.scalar.activation(y[:], acc[:], ACT.Copy, scale=inv_sum[:])
+            nc.sync.dma_start(out[0, :, h * P : (h + 1) * P], y[:])

@@ -1,7 +1,6 @@
 from contextlib import ExitStack
 
 import concourse.mybir as mybir
-from concourse.masks import make_identity
 
 N, T, D, DV, NQ = 512, 2048, 512, 256, 128
 FLOPS = 2 * NQ * N * (D + DV)
@@ -27,25 +26,33 @@ def tile_attend_soft_topk_kernel(tc, qT, k_words, k_scales, vT, vs, offs, out):
         sb = ctx.enter_context(tc.tile_pool(name="sb", bufs=1))
         ps = ctx.enter_context(tc.psum_pool(name="ps", bufs=1))
 
+        shared = ctx.enter_context(tc.tile_pool(name="shared", bufs=1))
+        pool_bytes = 4 * T
         offsets = sb.tile([P, N // 16], U16, name="offsets")
         q_raw = sb.tile([P, PACK, NQ], F32, name="q_raw")
-        key_pool = sb.tile([P, T], I32, name="key_pool", tag="slot_k", align_bytes=64)
-        key_scale_pool = sb.tile([P, T // 4], I32, name="key_scale_pool", tag="slot_s", align_bytes=64)
-        vs_pool = sb.tile([P, T], F32, name="vs_pool", tag="slot_v")
-        v_pool0 = sb.tile([P, T], F32, name="v_pool0")
+        key_scale_pool = sb.tile([P, T // 4], I32, name="key_scale_pool")
+        vs_pool = sb.tile([P, T], F32, name="vs_pool")
 
         nc.vector.memset(key_scale_pool[:], 0)
         nc.vector.memset(vs_pool[:VS_ROW, :], 0.0)
         nc.sync.dma_start(offsets[:], offs)
         nc.sync.dma_start(vs_pool[VS_ROW:, :], vs[0:1, :])
-        for quad in range(4):
-            nc.scalar.dma_start(key_scale_pool[32 * quad : 32 * quad + 4, :], k_scales[0, 4 * quad : 4 * quad + 4, :].bitcast(I32))
         nc.sync.dma_start(q_raw[:], qT[0].rearrange("(p t) q -> p t q", t=PACK))
+        for quad in range(4):
+            nc.sync.dma_start(key_scale_pool[32 * quad : 32 * quad + 4, :], k_scales[0, 4 * quad : 4 * quad + 4, :].bitcast(I32))
+
+        zeros = shared.tile([P, P], F32, name="zeros", offset=2 * pool_bytes - 2 * P)
+        ident = sb.tile([P, P], F32, name="ident")
+        nc.gpsimd.memset(zeros[:], 0.0)
+        nc.gpsimd.affine_select(out=ident[:], in_=zeros[:], compare_op=ALU.not_equal, fill=1.0, base=0,
+                                pattern=[[-1, P]], channel_multiplier=1)
+
+        key_pool = shared.tile([P, T], I32, name="key_pool", offset=0)
+        v_pool0 = shared.tile([P, T], F32, name="v_pool0", offset=pool_bytes)
         nc.sync.dma_start(key_pool[:], k_words[0].rearrange("p t r -> p (t r)").bitcast(I32))
         nc.sync.dma_start(v_pool0[:], vT[:P, :])
-
-        ident = sb.tile([P, P], F32, name="ident")
-        make_identity(nc, ident[:])
+        v_pool1 = shared.tile([P, T], F32, name="v_pool1", offset=2 * pool_bytes)
+        nc.sync.dma_start(v_pool1[:], vT[P:, :])
 
         key_scales = sb.tile([P, N], U8, name="key_scales", align_bytes=64)
         nc.vector.tensor_copy(key_scales[:], key_scale_pool[:].bitcast(U8).indirect(offsets[:]))
@@ -56,14 +63,11 @@ def tile_attend_soft_topk_kernel(tc, qT, k_words, k_scales, vT, vs, offs, out):
         vs_row = sb.tile([P, N], F32, name="vs_row")
         nc.vector.tensor_copy(vs_row[:], vs_pool[:].indirect(offsets[:]))
 
-        v_pool1 = sb.tile([P, T], F32, name="v_pool1", tag="slot_v")
-        nc.sync.dma_start(v_pool1[:], vT[P:, :])
-
         q_codes = sb.tile([P, NQ], U32, name="q_codes", align_bytes=64)
         q_scales = sb.tile([P, NQ], U8, name="q_scales", align_bytes=64)
         nc.vector.quantize_mx(out=q_codes[:].bitcast(FP8X4), scales=q_scales[:], in_=q_bf[:].rearrange("p q t -> p (q t)"))
 
-        key_codes = sb.tile([P, N], U32, name="key_codes", tag="slot_s", align_bytes=64)
+        key_codes = sb.tile([P, N], U32, name="key_codes", align_bytes=64)
         nc.vector.tensor_copy(key_codes[:], key_pool[:].bitcast(U32).indirect(offsets[:]))
 
         vs_turned = ps.tile([P, PACK, P], F32, name="vs_turned")
@@ -75,50 +79,55 @@ def tile_attend_soft_topk_kernel(tc, qT, k_words, k_scales, vT, vs, offs, out):
         scores = ps.tile([P, N], F32, name="scores")
         nc.tensor.matmul_mx(out=scores[:], lhsT=q_codes[:].bitcast(FP8X4), lhsT_scale=q_scales[:],
                             rhs=key_codes[:].bitcast(FP8X4), rhs_scale=key_scales[:], start=True, stop=True)
-        neg_max = sb.tile([P, 1], F32, name="neg_max")
-        nc.vector.tensor_reduce(neg_max[:], scores[:], mybir.AxisListType.X, ALU.max, negate=True)
 
-        def gather_values(v_pool, name, tag):
-            pairs = sb.tile([P, 2, P, 2], BF16, name=name, tag=tag, align_bytes=64)
-            nc.vector.tensor_copy(pairs[:].rearrange("f u p e -> f p u e"), v_pool[:].indirect(offsets[:]))
+        def gather_values(h):
+            pairs = shared.tile([P, 2, P, 2], BF16, name="v_pairs%d" % h, align_bytes=64, offset=3 * pool_bytes + 2048 * h)
+            nc.vector.tensor_copy(pairs[:].rearrange("f u p e -> f p u e"), (v_pool0, v_pool1)[h][:].indirect(offsets[:]))
             return pairs
 
         def turn_values(h, pairs):
             turned = ps.tile([P, 2, P], F32, name="v_turned%d" % h)
             for u in range(2):
                 nc.tensor.transpose(turned[:, u, :], pairs[:, u].rearrange("f p e -> f (p e)").bitcast(F32), ident[:])
+            return turned
+
+        def group_values(h, turned):
             grouped = sb.tile([P, P, 2], F32, name="v_grouped%d" % h, align_bytes=64)
             nc.scalar.copy(grouped[:], turned[:].rearrange("p u f -> p f u"))
             return grouped
 
         def quantize_values(h, grouped):
-            codes = sb.tile([P, P], U32, name="v_codes%d" % h, align_bytes=64)
+            codes = shared.tile([P, P], U32, name="v_codes%d" % h, align_bytes=64, offset=2 * pool_bytes + 1024 + 512 * h)
             scales = sb.tile([P, P], U8, name="v_scales%d" % h, align_bytes=64)
             nc.vector.quantize_mx(out=codes[:].bitcast(FP8X4), scales=scales[:],
                                   in_=grouped[:].rearrange("p f u -> p (f u)").bitcast(BF16))
             return codes, scales
 
-        pairs0 = gather_values(v_pool0, "v_pairs0", "slot_k")
+        pairs0 = gather_values(0)
+        neg_max = shared.tile([P, 1], F32, name="neg_max", offset=pool_bytes)
+        nc.vector.tensor_reduce(neg_max[:], scores[:], mybir.AxisListType.X, ALU.max, negate=True)
 
-        p_exp = sb.tile([P, PACK, P], F32, name="p_exp")
+        turned0 = turn_values(0, pairs0)
+
+        p_exp = shared.tile([P, PACK, P], F32, name="p_exp", offset=3 * pool_bytes)
         row_sum = sb.tile([P, 1], F32, name="row_sum")
         nc.scalar.activation(p_exp[:], scores[:].rearrange("q (p t) -> q t p", t=PACK), ACT.Exp, bias=neg_max[:], accum_out=row_sum[:])
         p_turned = ps.tile([P, PACK, NQ], F32, name="p_turned")
         for t in range(PACK):
             nc.tensor.transpose(p_turned[:, t, :], p_exp[:, t, :], ident[:])
-        grouped0 = turn_values(0, pairs0)
+        grouped0 = group_values(0, turned0)
 
-        pairs1 = gather_values(v_pool1, "v_pairs1", "v_pairs1")
-        grouped1 = turn_values(1, pairs1)
+        pairs1 = gather_values(1)
+        grouped1 = group_values(1, turn_values(1, pairs1))
 
-        w_bf = sb.tile([P, NQ, PACK], BF16, name="w_bf", align_bytes=64)
+        w_bf = shared.tile([P, NQ, PACK], BF16, name="w_bf", align_bytes=64, offset=2 * pool_bytes)
         nc.vector.tensor_tensor(w_bf[:], p_turned[:].rearrange("p t q -> p q t"),
                                 vs_slot[:].unsqueeze(1).to_broadcast([P, NQ, PACK]), ALU.mult)
         v0 = quantize_values(0, grouped0)
         w_codes = sb.tile([P, NQ], U32, name="w_codes", align_bytes=64)
         w_scales = sb.tile([P, NQ], U8, name="w_scales", align_bytes=64)
         nc.vector.quantize_mx(out=w_codes[:].bitcast(FP8X4), scales=w_scales[:], in_=w_bf[:].rearrange("p q t -> p (q t)"))
-        inv_sum = sb.tile([P, 1], F32, name="inv_sum")
+        inv_sum = shared.tile([P, 1], F32, name="inv_sum", offset=2 * pool_bytes + 2048)
         nc.vector.reciprocal(inv_sum[:], row_sum[:])
         v1 = quantize_values(1, grouped1)
 

@@ -31,20 +31,20 @@ def tile_attend_soft_topk_kernel(tc, qT, k_words, k_scales, vT, vs, offs, out):
         offsets = sb.tile([P, N // 16], U16, name="offsets")
         q_raw = sb.tile([P, PACK, NQ], F32, name="q_raw")
         key_scale_pool = sb.tile([P, T // 4], I32, name="key_scale_pool")
-        vs_pool = sb.tile([P, T], F32, name="vs_pool")
+        vs_pool = sb.tile([P, T + 1], F32, name="vs_pool")
 
         nc.vector.memset(key_scale_pool[:], 0)
         nc.vector.memset(vs_pool[:VS_ROW, :], 0.0)
         nc.sync.dma_start(offsets[:], offs)
-        nc.sync.dma_start(vs_pool[VS_ROW:, :], vs[0:1, :])
+        nc.sync.dma_start(vs_pool[VS_ROW:, :T], vs[0:1, :])
         nc.sync.dma_start(q_raw[:], qT[0].rearrange("(p t) q -> p t q", t=PACK))
         for quad in range(4):
             nc.sync.dma_start(key_scale_pool[32 * quad : 32 * quad + 4, :], k_scales[0, 4 * quad : 4 * quad + 4, :].bitcast(I32))
 
-        zeros = shared.tile([P, P], F32, name="zeros", offset=2 * pool_bytes - 2 * P)
+        zeros = shared.tile([P, T + 2 * P], F32, name="zeros", offset=pool_bytes - 4 * P)
         ident = sb.tile([P, P], F32, name="ident")
-        nc.gpsimd.memset(zeros[:], 0.0)
-        nc.gpsimd.affine_select(out=ident[:], in_=zeros[:], compare_op=ALU.not_equal, fill=1.0, base=0,
+        nc.gpsimd.memset(zeros[:, :P], 0.0)
+        nc.gpsimd.affine_select(out=ident[:], in_=zeros[:, :P], compare_op=ALU.not_equal, fill=1.0, base=0,
                                 pattern=[[-1, P]], channel_multiplier=1)
 
         key_pool = shared.tile([P, T], I32, name="key_pool", offset=0)
@@ -61,7 +61,7 @@ def tile_attend_soft_topk_kernel(tc, qT, k_words, k_scales, vT, vs, offs, out):
         nc.scalar.copy(q_bf[:], q_raw[:].rearrange("p t q -> p q t"))
 
         vs_row = sb.tile([P, N], F32, name="vs_row")
-        nc.vector.tensor_copy(vs_row[:], vs_pool[:].indirect(offsets[:]))
+        nc.vector.tensor_copy(vs_row[:], vs_pool[:, :T].indirect(offsets[:]))
 
         q_codes = sb.tile([P, NQ], U32, name="q_codes", align_bytes=64)
         q_scales = sb.tile([P, NQ], U8, name="q_scales", align_bytes=64)
@@ -81,7 +81,7 @@ def tile_attend_soft_topk_kernel(tc, qT, k_words, k_scales, vT, vs, offs, out):
                             rhs=key_codes[:].bitcast(FP8X4), rhs_scale=key_scales[:], start=True, stop=True)
 
         def gather_values(h):
-            pairs = shared.tile([P, 2, P, 2], BF16, name="v_pairs%d" % h, align_bytes=64, offset=3 * pool_bytes + 2048 * h)
+            pairs = sb.tile([P, 2, P, 2], BF16, name="v_pairs%d" % h, align_bytes=64)
             nc.vector.tensor_copy(pairs[:].rearrange("f u p e -> f p u e"), (v_pool0, v_pool1)[h][:].indirect(offsets[:]))
             return pairs
 
@@ -103,19 +103,18 @@ def tile_attend_soft_topk_kernel(tc, qT, k_words, k_scales, vT, vs, offs, out):
                                   in_=grouped[:].rearrange("p f u -> p (f u)").bitcast(BF16))
             return codes, scales
 
-        pairs0 = gather_values(0)
-        neg_max = shared.tile([P, 1], F32, name="neg_max", offset=pool_bytes)
+        neg_max = sb.tile([P, 1], F32, name="neg_max")
         nc.vector.tensor_reduce(neg_max[:], scores[:], mybir.AxisListType.X, ALU.max, negate=True)
 
-        turned0 = turn_values(0, pairs0)
+        pairs0 = gather_values(0)
 
-        p_exp = shared.tile([P, PACK, P], F32, name="p_exp", offset=3 * pool_bytes)
+        p_exp = sb.tile([P, PACK, P], F32, name="p_exp")
         row_sum = sb.tile([P, 1], F32, name="row_sum")
         nc.scalar.activation(p_exp[:], scores[:].rearrange("q (p t) -> q t p", t=PACK), ACT.Exp, bias=neg_max[:], accum_out=row_sum[:])
         p_turned = ps.tile([P, PACK, NQ], F32, name="p_turned")
         for t in range(PACK):
             nc.tensor.transpose(p_turned[:, t, :], p_exp[:, t, :], ident[:])
-        grouped0 = group_values(0, turned0)
+        grouped0 = group_values(0, turn_values(0, pairs0))
 
         pairs1 = gather_values(1)
         grouped1 = group_values(1, turn_values(1, pairs1))
@@ -136,5 +135,9 @@ def tile_attend_soft_topk_kernel(tc, qT, k_words, k_scales, vT, vs, offs, out):
             nc.tensor.matmul_mx(out=acc[:], lhsT=w_codes[:].bitcast(FP8X4), lhsT_scale=w_scales[:],
                                 rhs=codes[:].bitcast(FP8X4), rhs_scale=scales[:], start=True, stop=True)
             y = sb.tile([NQ, P], F32, name="y%d" % h)
-            nc.scalar.activation(y[:], acc[:], ACT.Copy, scale=inv_sum[:])
-            nc.sync.dma_start(out[0, :, h * P : (h + 1) * P], y[:])
+            if h == 0:
+                nc.vector.tensor_scalar(y[:], acc[:], inv_sum[:], None, ALU.mult)
+                nc.sync.dma_start(out[0, :, :P], y[:])
+            else:
+                nc.scalar.activation(y[:], acc[:], ACT.Copy, scale=inv_sum[:])
+                nc.scalar.dma_start(out[0, :, P:], y[:])

@@ -130,14 +130,13 @@ def tile_attend_soft_topk_kernel(tc, qT, k_words, k_scales, vT, vs, offs, out):
         nc.vector.reciprocal(inv_sum[:], row_sum[:])
         v1 = quantize_values(1, grouped1)
 
+        y = sb.tile([NQ, DV], F32, name="y")
         for h, (codes, scales) in enumerate((v0, v1)):
             acc = ps.tile([NQ, P], F32, name="acc%d" % h)
             nc.tensor.matmul_mx(out=acc[:], lhsT=w_codes[:].bitcast(FP8X4), lhsT_scale=w_scales[:],
                                 rhs=codes[:].bitcast(FP8X4), rhs_scale=scales[:], start=True, stop=True)
-            y = sb.tile([NQ, P], F32, name="y%d" % h)
             if h == 0:
-                nc.vector.tensor_scalar(y[:], acc[:], inv_sum[:], None, ALU.mult)
-                nc.sync.dma_start(out[0, :, :P], y[:])
+                nc.vector.tensor_scalar(y[:, :P], acc[:], inv_sum[:], None, ALU.mult)
             else:
-                nc.scalar.activation(y[:], acc[:], ACT.Copy, scale=inv_sum[:])
-                nc.scalar.dma_start(out[0, :, P:], y[:])
+                nc.scalar.activation(y[:, P:], acc[:], ACT.Copy, scale=inv_sum[:])
+        nc.sync.dma_start(out[0], y[:])

@@ -18,6 +18,8 @@ ALU = mybir.AluOpType
 P = 128
 PACK = 4
 VS_ROW = P - 1
+SCALE_ROWS = D // 32
+SCALE_ROW0 = P - SCALE_ROWS
 
 
 def tile_attend_soft_topk_kernel(tc, qT, k_words, k_scales, vT, vs, offs, out):
@@ -31,43 +33,45 @@ def tile_attend_soft_topk_kernel(tc, qT, k_words, k_scales, vT, vs, offs, out):
         offsets = sb.tile([P, N // 16], U16, name="offsets")
         q_raw = sb.tile([P, PACK, NQ], F32, name="q_raw")
         key_scale_pool = sb.tile([P, T // 4], I32, name="key_scale_pool")
-        vs_pool = sb.tile([P, T + 1], F32, name="vs_pool")
+        vs_pool = sb.tile([P, T], F32, name="vs_pool")
 
-        nc.vector.memset(key_scale_pool[:], 0)
+        nc.vector.memset(key_scale_pool[:SCALE_ROW0, :], 0)
         nc.vector.memset(vs_pool[:VS_ROW, :], 0.0)
+        nc.sync.dma_start(key_scale_pool[SCALE_ROW0:, :], k_scales[0].bitcast(I32))
         nc.sync.dma_start(offsets[:], offs)
-        nc.sync.dma_start(vs_pool[VS_ROW:, :T], vs[0:1, :])
+        nc.sync.dma_start(vs_pool[VS_ROW:, :], vs[0:1, :])
         nc.sync.dma_start(q_raw[:], qT[0].rearrange("(p t) q -> p t q", t=PACK))
-        for quad in range(4):
-            nc.sync.dma_start(key_scale_pool[32 * quad : 32 * quad + 4, :], k_scales[0, 4 * quad : 4 * quad + 4, :].bitcast(I32))
 
-        zeros = shared.tile([P, T + 2 * P], F32, name="zeros", offset=pool_bytes - 4 * P)
         ident = sb.tile([P, P], F32, name="ident")
-        nc.gpsimd.memset(zeros[:, :P], 0.0)
-        nc.gpsimd.affine_select(out=ident[:], in_=zeros[:, :P], compare_op=ALU.not_equal, fill=1.0, base=0,
+        nc.gpsimd.memset(ident[:], 0.0)
+        nc.gpsimd.affine_select(out=ident[:], in_=ident[:], compare_op=ALU.not_equal, fill=1.0, base=0,
                                 pattern=[[-1, P]], channel_multiplier=1)
+        key_scales = sb.tile([P, N // 4], I32, name="key_scales", align_bytes=64)
+        nc.gpsimd.memset(key_scales[:], 0)
 
-        key_pool = shared.tile([P, T], I32, name="key_pool", offset=0)
-        v_pool0 = shared.tile([P, T], F32, name="v_pool0", offset=pool_bytes)
+        key_pool = sb.tile([P, T], I32, name="key_pool")
+        v_pool0 = sb.tile([P, T], F32, name="v_pool0")
         nc.sync.dma_start(key_pool[:], k_words[0].rearrange("p t r -> p (t r)").bitcast(I32))
         nc.sync.dma_start(v_pool0[:], vT[:P, :])
         v_pool1 = shared.tile([P, T], F32, name="v_pool1", offset=2 * pool_bytes)
         nc.sync.dma_start(v_pool1[:], vT[P:, :])
 
-        key_scales = sb.tile([P, N], U8, name="key_scales", align_bytes=64)
-        nc.vector.tensor_copy(key_scales[:], key_scale_pool[:].bitcast(U8).indirect(offsets[:]))
-
         q_bf = sb.tile([P, NQ, PACK], BF16, name="q_bf", align_bytes=64)
         nc.scalar.copy(q_bf[:], q_raw[:].rearrange("p t q -> p q t"))
 
+        picked_scales = sb.tile([P, N // 4], I32, name="picked_scales")
+        nc.vector.tensor_copy(picked_scales[:].bitcast(U8), key_scale_pool[:].bitcast(U8).indirect(offsets[:]))
+        for quad in range(4):
+            nc.scalar.dma_start(key_scales[32 * quad : 32 * quad + 4, :], picked_scales[SCALE_ROW0 + 4 * quad : SCALE_ROW0 + 4 * quad + 4, :])
+
         vs_row = sb.tile([P, N], F32, name="vs_row")
-        nc.vector.tensor_copy(vs_row[:], vs_pool[:, :T].indirect(offsets[:]))
+        nc.vector.tensor_copy(vs_row[:], vs_pool[:].indirect(offsets[:]))
 
         q_codes = sb.tile([P, NQ], U32, name="q_codes", align_bytes=64)
         q_scales = sb.tile([P, NQ], U8, name="q_scales", align_bytes=64)
         nc.vector.quantize_mx(out=q_codes[:].bitcast(FP8X4), scales=q_scales[:], in_=q_bf[:].rearrange("p q t -> p (q t)"))
 
-        key_codes = sb.tile([P, N], U32, name="key_codes", align_bytes=64)
+        key_codes = shared.tile([P, N], U32, name="key_codes", align_bytes=64, offset=0)
         nc.vector.tensor_copy(key_codes[:], key_pool[:].bitcast(U32).indirect(offsets[:]))
 
         vs_turned = ps.tile([P, PACK, P], F32, name="vs_turned")
@@ -78,10 +82,10 @@ def tile_attend_soft_topk_kernel(tc, qT, k_words, k_scales, vT, vs, offs, out):
 
         scores = ps.tile([P, N], F32, name="scores")
         nc.tensor.matmul_mx(out=scores[:], lhsT=q_codes[:].bitcast(FP8X4), lhsT_scale=q_scales[:],
-                            rhs=key_codes[:].bitcast(FP8X4), rhs_scale=key_scales[:], start=True, stop=True)
+                            rhs=key_codes[:].bitcast(FP8X4), rhs_scale=key_scales[:].bitcast(U8), start=True, stop=True)
 
         def gather_values(h):
-            pairs = sb.tile([P, 2, P, 2], BF16, name="v_pairs%d" % h, align_bytes=64)
+            pairs = shared.tile([P, 2, P, 2], BF16, name="v_pairs%d" % h, align_bytes=64, offset=1024 * h)
             nc.vector.tensor_copy(pairs[:].rearrange("f u p e -> f p u e"), (v_pool0, v_pool1)[h][:].indirect(offsets[:]))
             return pairs
 

@@ -33,7 +33,7 @@ def tile_attend_soft_topk_kernel(tc, qT, k_words, k_scales, vT, vs, offs, out):
         offsets = sb.tile([P, N // 16], U16, name="offsets")
         q_raw = sb.tile([P, PACK, NQ], F32, name="q_raw")
         key_scale_pool = sb.tile([P, T // 4], I32, name="key_scale_pool")
-        vs_pool = sb.tile([P, T], F32, name="vs_pool")
+        vs_pool = shared.tile([P, T], F32, name="vs_pool", offset=2 * pool_bytes)
 
         nc.vector.memset(key_scale_pool[:SCALE_ROW0, :], 0)
         nc.vector.memset(vs_pool[:VS_ROW, :], 0.0)
@@ -47,14 +47,12 @@ def tile_attend_soft_topk_kernel(tc, qT, k_words, k_scales, vT, vs, offs, out):
         nc.gpsimd.affine_select(out=ident[:], in_=ident[:], compare_op=ALU.not_equal, fill=1.0, base=0,
                                 pattern=[[-1, P]], channel_multiplier=1)
         key_scales = sb.tile([P, N // 4], I32, name="key_scales", align_bytes=64)
-        nc.gpsimd.memset(key_scales[:], 0)
+        nc.vector.memset(key_scales[:], 0)
 
         key_pool = sb.tile([P, T], I32, name="key_pool")
         v_pool0 = sb.tile([P, T], F32, name="v_pool0")
         nc.sync.dma_start(key_pool[:], k_words[0].rearrange("p t r -> p (t r)").bitcast(I32))
         nc.sync.dma_start(v_pool0[:], vT[:P, :])
-        v_pool1 = shared.tile([P, T], F32, name="v_pool1", offset=2 * pool_bytes)
-        nc.sync.dma_start(v_pool1[:], vT[P:, :])
 
         q_bf = sb.tile([P, NQ, PACK], BF16, name="q_bf", align_bytes=64)
         nc.scalar.copy(q_bf[:], q_raw[:].rearrange("p t q -> p q t"))
@@ -62,41 +60,45 @@ def tile_attend_soft_topk_kernel(tc, qT, k_words, k_scales, vT, vs, offs, out):
         picked_scales = sb.tile([P, N // 4], I32, name="picked_scales")
         nc.vector.tensor_copy(picked_scales[:].bitcast(U8), key_scale_pool[:].bitcast(U8).indirect(offsets[:]))
         for quad in range(4):
-            nc.scalar.dma_start(key_scales[32 * quad : 32 * quad + 4, :], picked_scales[SCALE_ROW0 + 4 * quad : SCALE_ROW0 + 4 * quad + 4, :])
+            nc.sync.dma_start(key_scales[32 * quad : 32 * quad + 4, :], picked_scales[SCALE_ROW0 + 4 * quad : SCALE_ROW0 + 4 * quad + 4, :])
+        v_pool1 = shared.tile([P, T], F32, name="v_pool1", offset=2 * pool_bytes)
+        nc.sync.dma_start(v_pool1[:], vT[P:, :])
 
         vs_row = sb.tile([P, N], F32, name="vs_row")
         nc.vector.tensor_copy(vs_row[:], vs_pool[:].indirect(offsets[:]))
 
-        q_codes = sb.tile([P, NQ], U32, name="q_codes", align_bytes=64)
+        q_codes = shared.tile([P, NQ], U32, name="q_codes", align_bytes=64, offset=4 * N)
         q_scales = sb.tile([P, NQ], U8, name="q_scales", align_bytes=64)
         nc.vector.quantize_mx(out=q_codes[:].bitcast(FP8X4), scales=q_scales[:], in_=q_bf[:].rearrange("p q t -> p (q t)"))
 
         key_codes = shared.tile([P, N], U32, name="key_codes", align_bytes=64, offset=0)
         nc.vector.tensor_copy(key_codes[:], key_pool[:].bitcast(U32).indirect(offsets[:]))
 
-        vs_turned = ps.tile([P, PACK, P], F32, name="vs_turned")
+        vs_turned = ps.tile([P, PACK, P], F32, name="vs_turned", tag="turned0")
         for t in range(PACK):
             nc.tensor.transpose(vs_turned[:, t, :], vs_row[:, t:N:PACK], ident[:])
-        vs_slot = sb.tile([P, PACK], F32, name="vs_slot")
-        nc.scalar.copy(vs_slot[:], vs_turned[:, :, VS_ROW])
-
         scores = ps.tile([P, N], F32, name="scores")
         nc.tensor.matmul_mx(out=scores[:], lhsT=q_codes[:].bitcast(FP8X4), lhsT_scale=q_scales[:],
                             rhs=key_codes[:].bitcast(FP8X4), rhs_scale=key_scales[:].bitcast(U8), start=True, stop=True)
+        vs_slot = shared.tile([P, PACK], F32, name="vs_slot", offset=4 * N)
+        nc.scalar.copy(vs_slot[:], vs_turned[:, :, VS_ROW])
 
         def gather_values(h):
-            pairs = shared.tile([P, 2, P, 2], BF16, name="v_pairs%d" % h, align_bytes=64, offset=1024 * h)
+            if h == 0:
+                pairs = sb.tile([P, 2, P, 2], BF16, name="v_pairs0", align_bytes=64)
+            else:
+                pairs = shared.tile([P, 2, P, 2], BF16, name="v_pairs1", align_bytes=64, offset=0)
             nc.vector.tensor_copy(pairs[:].rearrange("f u p e -> f p u e"), (v_pool0, v_pool1)[h][:].indirect(offsets[:]))
             return pairs
 
         def turn_values(h, pairs):
-            turned = ps.tile([P, 2, P], F32, name="v_turned%d" % h)
+            turned = ps.tile([P, 2, P], F32, name="v_turned%d" % h, tag="turned%d" % h)
             for u in range(2):
                 nc.tensor.transpose(turned[:, u, :], pairs[:, u].rearrange("f p e -> f (p e)").bitcast(F32), ident[:])
             return turned
 
         def group_values(h, turned):
-            grouped = sb.tile([P, P, 2], F32, name="v_grouped%d" % h, align_bytes=64)
+            grouped = shared.tile([P, P, 2], F32, name="v_grouped%d" % h, align_bytes=64, offset=5 * N + 1024 * h)
             nc.scalar.copy(grouped[:], turned[:].rearrange("p u f -> p f u"))
             return grouped
 
@@ -107,18 +109,24 @@ def tile_attend_soft_topk_kernel(tc, qT, k_words, k_scales, vT, vs, offs, out):
                                   in_=grouped[:].rearrange("p f u -> p (f u)").bitcast(BF16))
             return codes, scales
 
-        neg_max = sb.tile([P, 1], F32, name="neg_max")
-        nc.vector.tensor_reduce(neg_max[:], scores[:], mybir.AxisListType.X, ALU.max, negate=True)
-
         pairs0 = gather_values(0)
 
+        turned0 = turn_values(0, pairs0)
+
+        neg_max = shared.tile([P, 1], F32, name="neg_max", offset=5 * N)
+        nc.vector.tensor_reduce(neg_max[:], scores[:], mybir.AxisListType.X, ALU.max, negate=True)
+
         p_exp = sb.tile([P, PACK, P], F32, name="p_exp")
-        row_sum = sb.tile([P, 1], F32, name="row_sum")
-        nc.scalar.activation(p_exp[:], scores[:].rearrange("q (p t) -> q t p", t=PACK), ACT.Exp, bias=neg_max[:], accum_out=row_sum[:])
+        part_sums = sb.tile([P, 2], F32, name="part_sums")
         p_turned = ps.tile([P, PACK, NQ], F32, name="p_turned")
-        for t in range(PACK):
-            nc.tensor.transpose(p_turned[:, t, :], p_exp[:, t, :], ident[:])
-        grouped0 = group_values(0, turn_values(0, pairs0))
+        for u in range(2):
+            nc.scalar.activation(p_exp[:, 2 * u : 2 * u + 2, :], scores[:].rearrange("q (p t) -> q t p", t=PACK)[:, 2 * u : 2 * u + 2, :],
+                                 ACT.Exp, bias=neg_max[:], accum_out=part_sums[:, u : u + 1])
+            for t in (2 * u, 2 * u + 1):
+                nc.tensor.transpose(p_turned[:, t, :], p_exp[:, t, :], ident[:])
+        grouped0 = group_values(0, turned0)
+        row_sum = sb.tile([P, 1], F32, name="row_sum")
+        nc.scalar.activation(row_sum[:], part_sums[:, 0:1], ACT.Identity, bias=part_sums[:, 1:2])
 
         pairs1 = gather_values(1)
         grouped1 = group_values(1, turn_values(1, pairs1))

@@ -148,7 +148,7 @@ def tile_attend_soft_topk_kernel(tc, qT, k_words, k_scales, vT, vs, offs, out):
             nc.tensor.matmul_mx(out=acc[:], lhsT=w_codes[:].bitcast(FP8X4), lhsT_scale=w_scales[:],
                                 rhs=codes[:].bitcast(FP8X4), rhs_scale=scales[:], start=True, stop=True)
             if h == 0:
-                nc.vector.tensor_scalar(y[:, :P], acc[:], inv_sum[:], None, ALU.mult)
+                nc.scalar.activation(y[:, :P], acc[:], ACT.Copy, scale=inv_sum[:])
             else:
-                nc.scalar.activation(y[:, P:], acc[:], ACT.Copy, scale=inv_sum[:])
-        nc.sync.dma_start(out[0], y[:])
+                nc.vector.tensor_scalar(y[:, P:], acc[:], inv_sum[:], None, ALU.mult)
+            nc.sync.dma_start(out[0][:, h * P : (h + 1) * P], y[:, h * P : (h + 1) * P])

@@ -20,6 +20,7 @@ PACK = 4
 VS_ROW = P - 1
 SCALE_ROWS = D // 32
 SCALE_ROW0 = P - SCALE_ROWS
+EARLY = 1024
 
 
 def tile_attend_soft_topk_kernel(tc, qT, k_words, k_scales, vT, vs, offs, out):
@@ -32,11 +33,10 @@ def tile_attend_soft_topk_kernel(tc, qT, k_words, k_scales, vT, vs, offs, out):
         pool_bytes = 4 * T
         offsets = sb.tile([P, N // 16], U16, name="offsets")
         q_raw = sb.tile([P, PACK, NQ], F32, name="q_raw")
-        key_scale_pool = sb.tile([P, T // 4], I32, name="key_scale_pool")
-        vs_pool = shared.tile([P, T], F32, name="vs_pool", offset=2 * pool_bytes)
+        key_scale_pool = shared.tile([P, T // 4], I32, name="key_scale_pool", offset=2 * pool_bytes - 1024)
+        vs_pool = shared.tile([P, T], F32, name="vs_pool", offset=3 * pool_bytes)
 
         nc.vector.memset(key_scale_pool[:SCALE_ROW0, :], 0)
-        nc.vector.memset(vs_pool[:VS_ROW, :], 0.0)
         nc.sync.dma_start(key_scale_pool[SCALE_ROW0:, :], k_scales[0].bitcast(I32))
         nc.sync.dma_start(offsets[:], offs)
         nc.sync.dma_start(vs_pool[VS_ROW:, :], vs[0:1, :])
@@ -46,13 +46,15 @@ def tile_attend_soft_topk_kernel(tc, qT, k_words, k_scales, vT, vs, offs, out):
         nc.gpsimd.memset(ident[:], 0.0)
         nc.gpsimd.affine_select(out=ident[:], in_=ident[:], compare_op=ALU.not_equal, fill=1.0, base=0,
                                 pattern=[[-1, P]], channel_multiplier=1)
+        nc.gpsimd.memset(vs_pool[:VS_ROW, :], 0.0)
         key_scales = sb.tile([P, N // 4], I32, name="key_scales", align_bytes=64)
         nc.vector.memset(key_scales[:], 0)
 
         key_pool = sb.tile([P, T], I32, name="key_pool")
-        v_pool0 = sb.tile([P, T], F32, name="v_pool0")
         nc.sync.dma_start(key_pool[:], k_words[0].rearrange("p t r -> p (t r)").bitcast(I32))
-        nc.sync.dma_start(v_pool0[:], vT[:P, :])
+
+        v_early = sb.tile([P, EARLY], F32, name="v_early")
+        nc.sync.dma_start(v_early[:], vT[:P, :EARLY])
 
         q_bf = sb.tile([P, NQ, PACK], BF16, name="q_bf", align_bytes=64)
         nc.scalar.copy(q_bf[:], q_raw[:].rearrange("p t q -> p q t"))
@@ -61,33 +63,33 @@ def tile_attend_soft_topk_kernel(tc, qT, k_words, k_scales, vT, vs, offs, out):
         nc.vector.tensor_copy(picked_scales[:].bitcast(U8), key_scale_pool[:].bitcast(U8).indirect(offsets[:]))
         for quad in range(4):
             nc.sync.dma_start(key_scales[32 * quad : 32 * quad + 4, :], picked_scales[SCALE_ROW0 + 4 * quad : SCALE_ROW0 + 4 * quad + 4, :])
+        v_pool0 = shared.tile([P, T], F32, name="v_pool0", offset=pool_bytes)
+        nc.sync.dma_start(v_pool0[:, EARLY:], vT[:P, EARLY:])
         v_pool1 = shared.tile([P, T], F32, name="v_pool1", offset=2 * pool_bytes)
         nc.sync.dma_start(v_pool1[:], vT[P:, :])
 
         vs_row = sb.tile([P, N], F32, name="vs_row")
         nc.vector.tensor_copy(vs_row[:], vs_pool[:].indirect(offsets[:]))
 
-        q_codes = shared.tile([P, NQ], U32, name="q_codes", align_bytes=64, offset=4 * N)
+        q_codes = sb.tile([P, NQ], U32, name="q_codes", align_bytes=64)
         q_scales = sb.tile([P, NQ], U8, name="q_scales", align_bytes=64)
         nc.vector.quantize_mx(out=q_codes[:].bitcast(FP8X4), scales=q_scales[:], in_=q_bf[:].rearrange("p q t -> p (q t)"))
 
-        key_codes = shared.tile([P, N], U32, name="key_codes", align_bytes=64, offset=0)
+        key_codes = shared.tile([P, N], U32, name="key_codes", align_bytes=64, offset=3 * pool_bytes)
         nc.vector.tensor_copy(key_codes[:], key_pool[:].bitcast(U32).indirect(offsets[:]))
 
-        vs_turned = ps.tile([P, PACK, P], F32, name="vs_turned", tag="turned0")
+        vs_turned = ps.tile([P, PACK, P], F32, name="vs_turned")
         for t in range(PACK):
             nc.tensor.transpose(vs_turned[:, t, :], vs_row[:, t:N:PACK], ident[:])
-        scores = ps.tile([P, N], F32, name="scores")
+        vs_slot = sb.tile([P, PACK], F32, name="vs_slot")
+        nc.scalar.copy(vs_slot[:], vs_turned[:, :, VS_ROW])
+        nc.scalar.copy(v_pool0[:, :EARLY], v_early[:])
+        scores = ps.tile([P, N], F32, name="scores", tag="turned1")
         nc.tensor.matmul_mx(out=scores[:], lhsT=q_codes[:].bitcast(FP8X4), lhsT_scale=q_scales[:],
                             rhs=key_codes[:].bitcast(FP8X4), rhs_scale=key_scales[:].bitcast(U8), start=True, stop=True)
-        vs_slot = shared.tile([P, PACK], F32, name="vs_slot", offset=4 * N)
-        nc.scalar.copy(vs_slot[:], vs_turned[:, :, VS_ROW])
 
         def gather_values(h):
-            if h == 0:
-                pairs = sb.tile([P, 2, P, 2], BF16, name="v_pairs0", align_bytes=64)
-            else:
-                pairs = shared.tile([P, 2, P, 2], BF16, name="v_pairs1", align_bytes=64, offset=0)
+            pairs = shared.tile([P, 2, P, 2], BF16, name="v_pairs%d" % h, align_bytes=64, offset=3 * pool_bytes + 1024 * h)
             nc.vector.tensor_copy(pairs[:].rearrange("f u p e -> f p u e"), (v_pool0, v_pool1)[h][:].indirect(offsets[:]))
             return pairs
 
@@ -98,7 +100,7 @@ def tile_attend_soft_topk_kernel(tc, qT, k_words, k_scales, vT, vs, offs, out):
             return turned
 
         def group_values(h, turned):
-            grouped = shared.tile([P, P, 2], F32, name="v_grouped%d" % h, align_bytes=64, offset=5 * N + 1024 * h)
+            grouped = shared.tile([P, P, 2], F32, name="v_grouped%d" % h, align_bytes=64, offset=1024 * h)
             nc.scalar.copy(grouped[:], turned[:].rearrange("p u f -> p f u"))
             return grouped
 
@@ -109,33 +111,27 @@ def tile_attend_soft_topk_kernel(tc, qT, k_words, k_scales, vT, vs, offs, out):
                                   in_=grouped[:].rearrange("p f u -> p (f u)").bitcast(BF16))
             return codes, scales
 
-        pairs0 = gather_values(0)
-
-        turned0 = turn_values(0, pairs0)
-
-        neg_max = shared.tile([P, 1], F32, name="neg_max", offset=5 * N)
+        neg_max = shared.tile([P, 1], F32, name="neg_max", offset=0)
         nc.vector.tensor_reduce(neg_max[:], scores[:], mybir.AxisListType.X, ALU.max, negate=True)
 
+        pairs0 = gather_values(0)
+
         p_exp = sb.tile([P, PACK, P], F32, name="p_exp")
-        part_sums = sb.tile([P, 2], F32, name="part_sums")
-        p_turned = ps.tile([P, PACK, NQ], F32, name="p_turned")
-        for u in range(2):
-            nc.scalar.activation(p_exp[:, 2 * u : 2 * u + 2, :], scores[:].rearrange("q (p t) -> q t p", t=PACK)[:, 2 * u : 2 * u + 2, :],
-                                 ACT.Exp, bias=neg_max[:], accum_out=part_sums[:, u : u + 1])
-            for t in (2 * u, 2 * u + 1):
-                nc.tensor.transpose(p_turned[:, t, :], p_exp[:, t, :], ident[:])
-        grouped0 = group_values(0, turned0)
         row_sum = sb.tile([P, 1], F32, name="row_sum")
-        nc.scalar.activation(row_sum[:], part_sums[:, 0:1], ACT.Identity, bias=part_sums[:, 1:2])
+        nc.scalar.activation(p_exp[:], scores[:].rearrange("q (p t) -> q t p", t=PACK), ACT.Exp, bias=neg_max[:], accum_out=row_sum[:])
+        p_turned = ps.tile([P, PACK, NQ], F32, name="p_turned")
+        for t in range(PACK):
+            nc.tensor.transpose(p_turned[:, t, :], p_exp[:, t, :], ident[:])
+        grouped0 = group_values(0, turn_values(0, pairs0))
 
         pairs1 = gather_values(1)
         grouped1 = group_values(1, turn_values(1, pairs1))
 
-        w_bf = shared.tile([P, NQ, PACK], BF16, name="w_bf", align_bytes=64, offset=2 * pool_bytes)
+        w_bf = shared.tile([P, NQ, PACK], BF16, name="w_bf", align_bytes=64, offset=2 * pool_bytes + 4096)
         nc.vector.tensor_tensor(w_bf[:], p_turned[:].rearrange("p t q -> p q t"),
                                 vs_slot[:].unsqueeze(1).to_broadcast([P, NQ, PACK]), ALU.mult)
         v0 = quantize_values(0, grouped0)
-        w_codes = sb.tile([P, NQ], U32, name="w_codes", align_bytes=64)
+        w_codes = shared.tile([P, NQ], U32, name="w_codes", align_bytes=64, offset=2 * pool_bytes)
         w_scales = sb.tile([P, NQ], U8, name="w_scales", align_bytes=64)
         nc.vector.quantize_mx(out=w_codes[:].bitcast(FP8X4), scales=w_scales[:], in_=w_bf[:].rearrange("p q t -> p (q t)"))
         inv_sum = shared.tile([P, 1], F32, name="inv_sum", offset=2 * pool_bytes + 2048)

@@ -37,6 +37,7 @@ def tile_attend_soft_topk_kernel(tc, qT, k_words, k_scales, vT, vs, offs, out):
         vs_pool = shared.tile([P, T], F32, name="vs_pool", offset=3 * pool_bytes)
 
         nc.vector.memset(key_scale_pool[:SCALE_ROW0, :], 0)
+        nc.vector.memset(vs_pool[:VS_ROW, :], 0.0)
         nc.sync.dma_start(key_scale_pool[SCALE_ROW0:, :], k_scales[0].bitcast(I32))
         nc.sync.dma_start(offsets[:], offs)
         nc.sync.dma_start(vs_pool[VS_ROW:, :], vs[0:1, :])
@@ -46,7 +47,6 @@ def tile_attend_soft_topk_kernel(tc, qT, k_words, k_scales, vT, vs, offs, out):
         nc.gpsimd.memset(ident[:], 0.0)
         nc.gpsimd.affine_select(out=ident[:], in_=ident[:], compare_op=ALU.not_equal, fill=1.0, base=0,
                                 pattern=[[-1, P]], channel_multiplier=1)
-        nc.gpsimd.memset(vs_pool[:VS_ROW, :], 0.0)
         key_scales = sb.tile([P, N // 4], I32, name="key_scales", align_bytes=64)
         nc.vector.memset(key_scales[:], 0)
 

@@ -21,6 +21,7 @@ VS_ROW = P - 1
 SCALE_ROWS = D // 32
 SCALE_ROW0 = P - SCALE_ROWS
 EARLY = 1024
+HALF = N // 2
 
 
 def tile_attend_soft_topk_kernel(tc, qT, k_words, k_scales, vT, vs, offs, out):
@@ -76,7 +77,9 @@ def tile_attend_soft_topk_kernel(tc, qT, k_words, k_scales, vT, vs, offs, out):
         nc.vector.quantize_mx(out=q_codes[:].bitcast(FP8X4), scales=q_scales[:], in_=q_bf[:].rearrange("p q t -> p (q t)"))
 
         key_codes = shared.tile([P, N], U32, name="key_codes", align_bytes=64, offset=3 * pool_bytes)
-        nc.vector.tensor_copy(key_codes[:], key_pool[:].bitcast(U32).indirect(offsets[:]))
+        for half in range(2):
+            nc.vector.tensor_copy(key_codes[:, half * HALF : (half + 1) * HALF],
+                                  key_pool[:].bitcast(U32).indirect(offsets[:, half * HALF // 16 : (half + 1) * HALF // 16]))
 
         vs_turned = ps.tile([P, PACK, P], F32, name="vs_turned")
         for t in range(PACK):
@@ -85,8 +88,10 @@ def tile_attend_soft_topk_kernel(tc, qT, k_words, k_scales, vT, vs, offs, out):
         nc.scalar.copy(vs_slot[:], vs_turned[:, :, VS_ROW])
         nc.scalar.copy(v_pool0[:, :EARLY], v_early[:])
         scores = ps.tile([P, N], F32, name="scores", tag="turned1")
-        nc.tensor.matmul_mx(out=scores[:], lhsT=q_codes[:].bitcast(FP8X4), lhsT_scale=q_scales[:],
-                            rhs=key_codes[:].bitcast(FP8X4), rhs_scale=key_scales[:].bitcast(U8), start=True, stop=True)
+        for half in range(2):
+            cols = slice(half * HALF, (half + 1) * HALF)
+            nc.tensor.matmul_mx(out=scores[:, cols], lhsT=q_codes[:].bitcast(FP8X4), lhsT_scale=q_scales[:],
+                                rhs=key_codes[:, cols].bitcast(FP8X4), rhs_scale=key_scales[:].bitcast(U8)[:, cols], start=True, stop=True)
 
         def gather_values(h):
             pairs = shared.tile([P, 2, P, 2], BF16, name="v_pairs%d" % h, align_bytes=64, offset=3 * pool_bytes + 1024 * h)

@@ -20,7 +20,7 @@ PACK = 4
 VS_ROW = P - 1
 SCALE_ROWS = D // 32
 SCALE_ROW0 = P - SCALE_ROWS
-EARLY = 1024
+EARLY = 1152
 HALF = N // 2
 
 
@@ -41,7 +41,7 @@ def tile_attend_soft_topk_kernel(tc, qT, k_words, k_scales, vT, vs, offs, out):
         nc.vector.memset(vs_pool[:VS_ROW, :], 0.0)
         nc.sync.dma_start(key_scale_pool[SCALE_ROW0:, :], k_scales[0].bitcast(I32))
         nc.sync.dma_start(offsets[:], offs)
-        nc.sync.dma_start(vs_pool[VS_ROW:, :], vs[0:1, :])
+        nc.scalar.dma_start(vs_pool[VS_ROW:, :], vs[0:1, :])
         nc.sync.dma_start(q_raw[:], qT[0].rearrange("(p t) q -> p t q", t=PACK))
 
         ident = sb.tile([P, P], F32, name="ident")

@@ -20,7 +20,7 @@ PACK = 4
 VS_ROW = P - 1
 SCALE_ROWS = D // 32
 SCALE_ROW0 = P - SCALE_ROWS
-EARLY = 1152
+EARLY = 1280
 HALF = N // 2
 
 
@@ -39,7 +39,7 @@ def tile_attend_soft_topk_kernel(tc, qT, k_words, k_scales, vT, vs, offs, out):
 
         nc.vector.memset(key_scale_pool[:SCALE_ROW0, :], 0)
         nc.vector.memset(vs_pool[:VS_ROW, :], 0.0)
-        nc.sync.dma_start(key_scale_pool[SCALE_ROW0:, :], k_scales[0].bitcast(I32))
+        nc.scalar.dma_start(key_scale_pool[SCALE_ROW0:, :], k_scales[0].bitcast(I32))
         nc.sync.dma_start(offsets[:], offs)
         nc.scalar.dma_start(vs_pool[VS_ROW:, :], vs[0:1, :])
         nc.sync.dma_start(q_raw[:], qT[0].rearrange("(p t) q -> p t q", t=PACK))

@@ -22,6 +22,7 @@ SCALE_ROWS = D // 32
 SCALE_ROW0 = P - SCALE_ROWS
 EARLY = 1280
 HALF = N // 2
+PART = P // 2
 
 
 def tile_attend_soft_topk_kernel(tc, qT, k_words, k_scales, vT, vs, offs, out):
@@ -69,8 +70,8 @@ def tile_attend_soft_topk_kernel(tc, qT, k_words, k_scales, vT, vs, offs, out):
         v_pool1 = shared.tile([P, T], F32, name="v_pool1", offset=2 * pool_bytes)
         nc.sync.dma_start(v_pool1[:], vT[P:, :])
 
-        vs_row = sb.tile([P, N], F32, name="vs_row")
-        nc.vector.tensor_copy(vs_row[:], vs_pool[:].indirect(offsets[:]))
+        vs_row = sb.tile([P, PACK, P], F32, name="vs_row")
+        nc.vector.tensor_copy(vs_row[:].bitcast(U32).rearrange("r t p -> r p t"), vs_pool[:].bitcast(U32).indirect(offsets[:]))
 
         q_codes = sb.tile([P, NQ], U32, name="q_codes", align_bytes=64)
         q_scales = sb.tile([P, NQ], U8, name="q_scales", align_bytes=64)
@@ -83,11 +84,11 @@ def tile_attend_soft_topk_kernel(tc, qT, k_words, k_scales, vT, vs, offs, out):
 
         vs_turned = ps.tile([P, PACK, P], F32, name="vs_turned")
         for t in range(PACK):
-            nc.tensor.transpose(vs_turned[:, t, :], vs_row[:, t:N:PACK], ident[:])
+            nc.tensor.transpose(vs_turned[:, t, :], vs_row[:, t, :], ident[:])
         vs_slot = sb.tile([P, PACK], F32, name="vs_slot")
         nc.scalar.copy(vs_slot[:], vs_turned[:, :, VS_ROW])
         nc.scalar.copy(v_pool0[:, :EARLY], v_early[:])
-        scores = ps.tile([P, N], F32, name="scores", tag="turned1")
+        scores = ps.tile([P, N], F32, name="scores", tag="turned0")
         for half in range(2):
             cols = slice(half * HALF, (half + 1) * HALF)
             nc.tensor.matmul_mx(out=scores[:, cols], lhsT=q_codes[:].bitcast(FP8X4), lhsT_scale=q_scales[:],
@@ -127,29 +128,42 @@ def tile_attend_soft_topk_kernel(tc, qT, k_words, k_scales, vT, vs, offs, out):
         p_turned = ps.tile([P, PACK, NQ], F32, name="p_turned")
         for t in range(PACK):
             nc.tensor.transpose(p_turned[:, t, :], p_exp[:, t, :], ident[:])
+        w_planes = sb.tile([P, PACK, NQ], F32, name="w_planes")
+        for t in range(PACK):
+            nc.scalar.activation(w_planes[:, t, :], p_turned[:, t, :], ACT.Copy, scale=vs_slot[:, t : t + 1])
         grouped0 = group_values(0, turn_values(0, pairs0))
 
         pairs1 = gather_values(1)
-        grouped1 = group_values(1, turn_values(1, pairs1))
+        turned1 = turn_values(1, pairs1)
+        grouped1 = [shared.tile([P, PART, 2], F32, name="v_grouped1_%d" % j, align_bytes=64, offset=1024 + 512 * j) for j in range(2)]
+        for j in range(2):
+            nc.scalar.copy(grouped1[j][:], turned1[:, :, j * PART : (j + 1) * PART].rearrange("p u f -> p f u"))
 
         w_bf = shared.tile([P, NQ, PACK], BF16, name="w_bf", align_bytes=64, offset=2 * pool_bytes + 4096)
-        nc.vector.tensor_tensor(w_bf[:], p_turned[:].rearrange("p t q -> p q t"),
-                                vs_slot[:].unsqueeze(1).to_broadcast([P, NQ, PACK]), ALU.mult)
-        v0 = quantize_values(0, grouped0)
+        nc.vector.tensor_copy(w_bf[:], w_planes[:].rearrange("p t q -> p q t"))
+        v0_codes, v0_scales = quantize_values(0, grouped0)
         w_codes = shared.tile([P, NQ], U32, name="w_codes", align_bytes=64, offset=2 * pool_bytes)
         w_scales = sb.tile([P, NQ], U8, name="w_scales", align_bytes=64)
         nc.vector.quantize_mx(out=w_codes[:].bitcast(FP8X4), scales=w_scales[:], in_=w_bf[:].rearrange("p q t -> p (q t)"))
         inv_sum = shared.tile([P, 1], F32, name="inv_sum", offset=2 * pool_bytes + 2048)
         nc.vector.reciprocal(inv_sum[:], row_sum[:])
-        v1 = quantize_values(1, grouped1)
+        v1_codes = shared.tile([P, P], U32, name="v_codes1", align_bytes=64, offset=2 * pool_bytes + 1024 + 512)
+        v1_scales = sb.tile([P, P], U8, name="v_scales1", align_bytes=64)
+        for j in range(2):
+            cols = slice(j * PART, (j + 1) * PART)
+            nc.vector.quantize_mx(out=v1_codes[:, cols].bitcast(FP8X4), scales=v1_scales[:, cols],
+                                  in_=grouped1[j][:].rearrange("p f u -> p (f u)").bitcast(BF16))
 
         y = sb.tile([NQ, DV], F32, name="y")
-        for h, (codes, scales) in enumerate((v0, v1)):
-            acc = ps.tile([NQ, P], F32, name="acc%d" % h)
+        parts = ((v0_codes[:], v0_scales[:], 0, P), (v1_codes[:, :PART], v1_scales[:, :PART], P, PART),
+                 (v1_codes[:, PART:], v1_scales[:, PART:], P + PART, PART))
+        for h, (codes, scales, first, width) in enumerate(parts):
+            acc = ps.tile([NQ, width], F32, name="acc%d" % h)
             nc.tensor.matmul_mx(out=acc[:], lhsT=w_codes[:].bitcast(FP8X4), lhsT_scale=w_scales[:],
-                                rhs=codes[:].bitcast(FP8X4), rhs_scale=scales[:], start=True, stop=True)
+                                rhs=codes.bitcast(FP8X4), rhs_scale=scales, start=True, stop=True)
             if h == 0:
-                nc.scalar.activation(y[:, :P], acc[:], ACT.Copy, scale=inv_sum[:])
+                nc.scalar.activation(y[:, first : first + width], acc[:], ACT.Copy, scale=inv_sum[:])
             else:
-                nc.vector.tensor_scalar(y[:, P:], acc[:], inv_sum[:], None, ALU.mult)
-            nc.sync.dma_start(out[0][:, h * P : (h + 1) * P], y[:, h * P : (h + 1) * P])
+                nc.vector.tensor_scalar(y[:, first : first + width], acc[:], inv_sum[:], None, ALU.mult)
+        nc.sync.dma_start(out[0][:, :P], y[:, :P])
+        nc.sync.dma_start(out[0][:, P:], y[:, P:])

@@ -123,14 +123,18 @@ def tile_attend_soft_topk_kernel(tc, qT, k_words, k_scales, vT, vs, offs, out):
         pairs0 = gather_values(0)
 
         p_exp = sb.tile([P, PACK, P], F32, name="p_exp")
-        row_sum = sb.tile([P, 1], F32, name="row_sum")
-        nc.scalar.activation(p_exp[:], scores[:].rearrange("q (p t) -> q t p", t=PACK), ACT.Exp, bias=neg_max[:], accum_out=row_sum[:])
-        p_turned = ps.tile([P, PACK, NQ], F32, name="p_turned")
+        part_sums = [sb.tile([P, 1], F32, name="part_sum%d" % u) for u in range(2)]
+        by_place = scores[:].rearrange("q (p t) -> q t p", t=PACK)
+        for u in range(2):
+            nc.scalar.activation(p_exp[:, 2 * u : 2 * u + 2, :], by_place[:, 2 * u : 2 * u + 2, :], ACT.Exp, bias=neg_max[:], accum_out=part_sums[u][:])
+        p_turned = [ps.tile([P, 2, NQ], F32, name="p_turned%d" % u) for u in range(2)]
         for t in range(PACK):
-            nc.tensor.transpose(p_turned[:, t, :], p_exp[:, t, :], ident[:])
+            nc.tensor.transpose(p_turned[t // 2][:, t % 2, :], p_exp[:, t, :], ident[:])
         w_planes = sb.tile([P, PACK, NQ], F32, name="w_planes")
         for t in range(PACK):
-            nc.scalar.activation(w_planes[:, t, :], p_turned[:, t, :], ACT.Copy, scale=vs_slot[:, t : t + 1])
+            nc.scalar.activation(w_planes[:, t, :], p_turned[t // 2][:, t % 2, :], ACT.Copy, scale=vs_slot[:, t : t + 1])
+        row_sum = sb.tile([P, 1], F32, name="row_sum")
+        nc.scalar.activation(row_sum[:], part_sums[0][:], ACT.Identity, bias=part_sums[1][:])
         grouped0 = group_values(0, turn_values(0, pairs0))
 
         pairs1 = gather_values(1)

@@ -22,6 +22,7 @@ SCALE_ROWS = D // 32
 SCALE_ROW0 = P - SCALE_ROWS
 EARLY = 1280
 HALF = N // 2
+SPLIT = 320
 PART = P // 2
 
 
@@ -34,7 +35,7 @@ def tile_attend_soft_topk_kernel(tc, qT, k_words, k_scales, vT, vs, offs, out):
         shared = ctx.enter_context(tc.tile_pool(name="shared", bufs=1))
         pool_bytes = 4 * T
         offsets = sb.tile([P, N // 16], U16, name="offsets")
-        q_raw = sb.tile([P, PACK, NQ], F32, name="q_raw")
+        q_raw = shared.tile([P, PACK, NQ], F32, name="q_raw", offset=5 * pool_bytes)
         key_scale_pool = shared.tile([P, T // 4], I32, name="key_scale_pool", offset=2 * pool_bytes - 1024)
         vs_pool = shared.tile([P, T], F32, name="vs_pool", offset=3 * pool_bytes)
 
@@ -70,43 +71,45 @@ def tile_attend_soft_topk_kernel(tc, qT, k_words, k_scales, vT, vs, offs, out):
         v_pool1 = shared.tile([P, T], F32, name="v_pool1", offset=2 * pool_bytes)
         nc.sync.dma_start(v_pool1[:], vT[P:, :])
 
-        vs_row = sb.tile([P, PACK, P], F32, name="vs_row")
-        nc.vector.tensor_copy(vs_row[:].bitcast(U32).rearrange("r t p -> r p t"), vs_pool[:].bitcast(U32).indirect(offsets[:]))
+        vs_row = shared.tile([P, P, PACK], F32, name="vs_row", offset=5 * pool_bytes)
+        nc.scalar.activation(vs_row[:].rearrange("r p t -> r (p t)"), vs_pool[:].indirect(offsets[:]), ACT.Copy)
 
         q_codes = sb.tile([P, NQ], U32, name="q_codes", align_bytes=64)
         q_scales = sb.tile([P, NQ], U8, name="q_scales", align_bytes=64)
         nc.vector.quantize_mx(out=q_codes[:].bitcast(FP8X4), scales=q_scales[:], in_=q_bf[:].rearrange("p q t -> p (q t)"))
 
-        key_codes = shared.tile([P, N], U32, name="key_codes", align_bytes=64, offset=3 * pool_bytes)
+        key_codes = shared.tile([P, N], U32, name="key_codes", align_bytes=64, offset=4 * pool_bytes)
         for half in range(2):
             nc.vector.tensor_copy(key_codes[:, half * HALF : (half + 1) * HALF],
                                   key_pool[:].bitcast(U32).indirect(offsets[:, half * HALF // 16 : (half + 1) * HALF // 16]))
 
         vs_turned = ps.tile([P, PACK, P], F32, name="vs_turned")
         for t in range(PACK):
-            nc.tensor.transpose(vs_turned[:, t, :], vs_row[:, t, :], ident[:])
-        vs_slot = sb.tile([P, PACK], F32, name="vs_slot")
-        nc.scalar.copy(vs_slot[:], vs_turned[:, :, VS_ROW])
+            nc.tensor.transpose(vs_turned[:, t, :], vs_row[:, :, t], ident[:])
+        vs_slot = sb.tile([P, 1, PACK], F32, name="vs_slot")
+        nc.scalar.copy(vs_slot[:, 0, :], vs_turned[:, :, VS_ROW])
         nc.scalar.copy(v_pool0[:, :EARLY], v_early[:])
-        scores = ps.tile([P, N], F32, name="scores", tag="turned0")
+        scores = ps.tile([P, N], F32, name="scores")
         for half in range(2):
             cols = slice(half * HALF, (half + 1) * HALF)
             nc.tensor.matmul_mx(out=scores[:, cols], lhsT=q_codes[:].bitcast(FP8X4), lhsT_scale=q_scales[:],
                                 rhs=key_codes[:, cols].bitcast(FP8X4), rhs_scale=key_scales[:].bitcast(U8)[:, cols], start=True, stop=True)
 
         def gather_values(h):
-            pairs = shared.tile([P, 2, P, 2], BF16, name="v_pairs%d" % h, align_bytes=64, offset=3 * pool_bytes + 1024 * h)
-            nc.vector.tensor_copy(pairs[:].rearrange("f u p e -> f p u e"), (v_pool0, v_pool1)[h][:].indirect(offsets[:]))
+            pairs = shared.tile([P, N], BF16, name="v_pairs%d" % h, align_bytes=64, offset=4 * pool_bytes + 1024 * h)
+            pool = (v_pool0, v_pool1)[h]
+            nc.vector.tensor_copy(pairs[:, :SPLIT], pool[:].indirect(offsets[:, : SPLIT // 16]))
+            nc.scalar.activation(pairs[:, SPLIT:], pool[:].indirect(offsets[:, SPLIT // 16 :]), ACT.Copy)
             return pairs
 
         def turn_values(h, pairs):
             turned = ps.tile([P, 2, P], F32, name="v_turned%d" % h, tag="turned%d" % h)
             for u in range(2):
-                nc.tensor.transpose(turned[:, u, :], pairs[:, u].rearrange("f p e -> f (p e)").bitcast(F32), ident[:])
+                nc.tensor.transpose(turned[:, u, :], pairs[:].bitcast(F32)[:, u::2], ident[:])
             return turned
 
         def group_values(h, turned):
-            grouped = shared.tile([P, P, 2], F32, name="v_grouped%d" % h, align_bytes=64, offset=1024 * h)
+            grouped = shared.tile([P, P, 2], F32, name="v_grouped%d" % h, align_bytes=64, offset=2 * pool_bytes + 5120)
             nc.scalar.copy(grouped[:], turned[:].rearrange("p u f -> p f u"))
             return grouped
 
@@ -117,7 +120,7 @@ def tile_attend_soft_topk_kernel(tc, qT, k_words, k_scales, vT, vs, offs, out):
                                   in_=grouped[:].rearrange("p f u -> p (f u)").bitcast(BF16))
             return codes, scales
 
-        neg_max = shared.tile([P, 1], F32, name="neg_max", offset=0)
+        neg_max = shared.tile([P, 1], F32, name="neg_max", offset=4 * pool_bytes + 1024)
         nc.vector.tensor_reduce(neg_max[:], scores[:], mybir.AxisListType.X, ALU.max, negate=True)
 
         pairs0 = gather_values(0)
@@ -127,12 +130,9 @@ def tile_attend_soft_topk_kernel(tc, qT, k_words, k_scales, vT, vs, offs, out):
         by_place = scores[:].rearrange("q (p t) -> q t p", t=PACK)
         for u in range(2):
             nc.scalar.activation(p_exp[:, 2 * u : 2 * u + 2, :], by_place[:, 2 * u : 2 * u + 2, :], ACT.Exp, bias=neg_max[:], accum_out=part_sums[u][:])
-        p_turned = [ps.tile([P, 2, NQ], F32, name="p_turned%d" % u) for u in range(2)]
+        p_turned = ps.tile([P, PACK, NQ], F32, name="p_turned")
         for t in range(PACK):
-            nc.tensor.transpose(p_turned[t // 2][:, t % 2, :], p_exp[:, t, :], ident[:])
-        w_planes = sb.tile([P, PACK, NQ], F32, name="w_planes")
-        for t in range(PACK):
-            nc.scalar.activation(w_planes[:, t, :], p_turned[t // 2][:, t % 2, :], ACT.Copy, scale=vs_slot[:, t : t + 1])
+            nc.tensor.transpose(p_turned[:, t, :], p_exp[:, t, :], ident[:])
         row_sum = sb.tile([P, 1], F32, name="row_sum")
         nc.scalar.activation(row_sum[:], part_sums[0][:], ACT.Identity, bias=part_sums[1][:])
         grouped0 = group_values(0, turn_values(0, pairs0))
@@ -144,7 +144,7 @@ def tile_attend_soft_topk_kernel(tc, qT, k_words, k_scales, vT, vs, offs, out):
             nc.scalar.copy(grouped1[j][:], turned1[:, :, j * PART : (j + 1) * PART].rearrange("p u f -> p f u"))
 
         w_bf = shared.tile([P, NQ, PACK], BF16, name="w_bf", align_bytes=64, offset=2 * pool_bytes + 4096)
-        nc.vector.tensor_copy(w_bf[:], w_planes[:].rearrange("p t q -> p q t"))
+        nc.vector.tensor_tensor(w_bf[:], p_turned[:].rearrange("p t q -> p q t"), vs_slot[:].to_broadcast([P, NQ, PACK]), ALU.mult)
         v0_codes, v0_scales = quantize_values(0, grouped0)
         w_codes = shared.tile([P, NQ], U32, name="w_codes", align_bytes=64, offset=2 * pool_bytes)
         w_scales = sb.tile([P, NQ], U8, name="w_scales", align_bytes=64)

@@ -22,7 +22,7 @@ SCALE_ROWS = D // 32
 SCALE_ROW0 = P - SCALE_ROWS
 EARLY = 1280
 HALF = N // 2
-SPLIT = 320
+SPLIT = 288
 PART = P // 2
 
 
@@ -89,7 +89,7 @@ def tile_attend_soft_topk_kernel(tc, qT, k_words, k_scales, vT, vs, offs, out):
         vs_slot = sb.tile([P, 1, PACK], F32, name="vs_slot")
         nc.scalar.copy(vs_slot[:, 0, :], vs_turned[:, :, VS_ROW])
         nc.scalar.copy(v_pool0[:, :EARLY], v_early[:])
-        scores = ps.tile([P, N], F32, name="scores")
+        scores = ps.tile([P, N], F32, name="scores", tag="turned0")
         for half in range(2):
             cols = slice(half * HALF, (half + 1) * HALF)
             nc.tensor.matmul_mx(out=scores[:, cols], lhsT=q_codes[:].bitcast(FP8X4), lhsT_scale=q_scales[:],

@@ -20,7 +20,7 @@ PACK = 4
 VS_ROW = P - 1
 SCALE_ROWS = D // 32
 SCALE_ROW0 = P - SCALE_ROWS
-EARLY = 1280
+EARLY = 960
 HALF = N // 2
 SPLIT = 288
 PART = P // 2
@@ -95,17 +95,10 @@ def tile_attend_soft_topk_kernel(tc, qT, k_words, k_scales, vT, vs, offs, out):
             nc.tensor.matmul_mx(out=scores[:, cols], lhsT=q_codes[:].bitcast(FP8X4), lhsT_scale=q_scales[:],
                                 rhs=key_codes[:, cols].bitcast(FP8X4), rhs_scale=key_scales[:].bitcast(U8)[:, cols], start=True, stop=True)
 
-        def gather_values(h):
-            pairs = shared.tile([P, N], BF16, name="v_pairs%d" % h, align_bytes=64, offset=4 * pool_bytes + 1024 * h)
-            pool = (v_pool0, v_pool1)[h]
-            nc.vector.tensor_copy(pairs[:, :SPLIT], pool[:].indirect(offsets[:, : SPLIT // 16]))
-            nc.scalar.activation(pairs[:, SPLIT:], pool[:].indirect(offsets[:, SPLIT // 16 :]), ACT.Copy)
-            return pairs
-
-        def turn_values(h, pairs):
+        def turn_values(h, halves):
             turned = ps.tile([P, 2, P], F32, name="v_turned%d" % h, tag="turned%d" % h)
             for u in range(2):
-                nc.tensor.transpose(turned[:, u, :], pairs[:].bitcast(F32)[:, u::2], ident[:])
+                nc.tensor.transpose(turned[:, u, :], halves[u], ident[:])
             return turned
 
         def group_values(h, turned):
@@ -123,7 +116,8 @@ def tile_attend_soft_topk_kernel(tc, qT, k_words, k_scales, vT, vs, offs, out):
         neg_max = shared.tile([P, 1], F32, name="neg_max", offset=4 * pool_bytes + 1024)
         nc.vector.tensor_reduce(neg_max[:], scores[:], mybir.AxisListType.X, ALU.max, negate=True)
 
-        pairs0 = gather_values(0)
+        pairs0 = shared.tile([P, 2, P, 2], BF16, name="v_pairs0", align_bytes=64, offset=4 * pool_bytes)
+        nc.vector.tensor_copy(pairs0[:].rearrange("f u p e -> f p u e"), v_pool0[:].indirect(offsets[:]))
 
         p_exp = sb.tile([P, PACK, P], F32, name="p_exp")
         part_sums = [sb.tile([P, 1], F32, name="part_sum%d" % u) for u in range(2)]
@@ -135,10 +129,12 @@ def tile_attend_soft_topk_kernel(tc, qT, k_words, k_scales, vT, vs, offs, out):
             nc.tensor.transpose(p_turned[:, t, :], p_exp[:, t, :], ident[:])
         row_sum = sb.tile([P, 1], F32, name="row_sum")
         nc.scalar.activation(row_sum[:], part_sums[0][:], ACT.Identity, bias=part_sums[1][:])
-        grouped0 = group_values(0, turn_values(0, pairs0))
+        grouped0 = group_values(0, turn_values(0, [pairs0[:, u].rearrange("f p e -> f (p e)").bitcast(F32) for u in range(2)]))
 
-        pairs1 = gather_values(1)
-        turned1 = turn_values(1, pairs1)
+        pairs1 = shared.tile([P, N], BF16, name="v_pairs1", align_bytes=64, offset=4 * pool_bytes + 1024)
+        nc.vector.tensor_copy(pairs1[:, :SPLIT], v_pool1[:].indirect(offsets[:, : SPLIT // 16]))
+        nc.scalar.activation(pairs1[:, SPLIT:], v_pool1[:].indirect(offsets[:, SPLIT // 16 :]), ACT.Copy)
+        turned1 = turn_values(1, [pairs1[:].bitcast(F32)[:, u::2] for u in range(2)])
         grouped1 = [shared.tile([P, PART, 2], F32, name="v_grouped1_%d" % j, align_bytes=64, offset=1024 + 512 * j) for j in range(2)]
         for j in range(2):
             nc.scalar.copy(grouped1[j][:], turned1[:, :, j * PART : (j + 1) * PART].rearrange("p u f -> p f u"))

@@ -22,7 +22,7 @@ SCALE_ROWS = D // 32
 SCALE_ROW0 = P - SCALE_ROWS
 EARLY = 960
 HALF = N // 2
-SPLIT = 288
+SPLIT = 256
 PART = P // 2
 
 
@@ -145,7 +145,7 @@ def tile_attend_soft_topk_kernel(tc, qT, k_words, k_scales, vT, vs, offs, out):
         w_codes = shared.tile([P, NQ], U32, name="w_codes", align_bytes=64, offset=2 * pool_bytes)
         w_scales = sb.tile([P, NQ], U8, name="w_scales", align_bytes=64)
         nc.vector.quantize_mx(out=w_codes[:].bitcast(FP8X4), scales=w_scales[:], in_=w_bf[:].rearrange("p q t -> p (q t)"))
-        inv_sum = shared.tile([P, 1], F32, name="inv_sum", offset=2 * pool_bytes + 2048)
+        inv_sum = shared.tile([P, 1], F32, name="inv_sum", offset=pool_bytes)
         nc.vector.reciprocal(inv_sum[:], row_sum[:])
         v1_codes = shared.tile([P, P], U32, name="v_codes1", align_bytes=64, offset=2 * pool_bytes + 1024 + 512)
         v1_scales = sb.tile([P, P], U8, name="v_scales1", align_bytes=64)

@@ -34,7 +34,7 @@ def tile_attend_soft_topk_kernel(tc, qT, k_words, k_scales, vT, vs, offs, out):
 
         shared = ctx.enter_context(tc.tile_pool(name="shared", bufs=1))
         pool_bytes = 4 * T
-        offsets = sb.tile([P, N // 16], U16, name="offsets")
+        offsets = sb.tile([P, N // 16], U16, name="offsets", align_bytes=256)
         q_raw = shared.tile([P, PACK, NQ], F32, name="q_raw", offset=5 * pool_bytes)
         key_scale_pool = shared.tile([P, T // 4], I32, name="key_scale_pool", offset=2 * pool_bytes - 1024)
         vs_pool = shared.tile([P, T], F32, name="vs_pool", offset=3 * pool_bytes)
@@ -50,19 +50,19 @@ def tile_attend_soft_topk_kernel(tc, qT, k_words, k_scales, vT, vs, offs, out):
         nc.gpsimd.memset(ident[:], 0.0)
         nc.gpsimd.affine_select(out=ident[:], in_=ident[:], compare_op=ALU.not_equal, fill=1.0, base=0,
                                 pattern=[[-1, P]], channel_multiplier=1)
-        key_scales = sb.tile([P, N // 4], I32, name="key_scales", align_bytes=64)
+        key_scales = sb.tile([P, N // 4], I32, name="key_scales", align_bytes=256)
         nc.vector.memset(key_scales[:], 0)
 
-        key_pool = sb.tile([P, T], I32, name="key_pool")
+        key_pool = sb.tile([P, T], I32, name="key_pool", align_bytes=256)
         nc.sync.dma_start(key_pool[:], k_words[0].rearrange("p t r -> p (t r)").bitcast(I32))
 
-        v_early = sb.tile([P, EARLY], F32, name="v_early")
+        v_early = sb.tile([P, EARLY], F32, name="v_early", align_bytes=256)
         nc.sync.dma_start(v_early[:], vT[:P, :EARLY])
 
-        q_bf = sb.tile([P, NQ, PACK], BF16, name="q_bf", align_bytes=64)
+        q_bf = sb.tile([P, NQ, PACK], BF16, name="q_bf", align_bytes=256)
         nc.scalar.copy(q_bf[:], q_raw[:].rearrange("p t q -> p q t"))
 
-        picked_scales = sb.tile([P, N // 4], I32, name="picked_scales")
+        picked_scales = sb.tile([P, N // 4], I32, name="picked_scales", align_bytes=256)
         nc.vector.tensor_copy(picked_scales[:].bitcast(U8), key_scale_pool[:].bitcast(U8).indirect(offsets[:]))
         for quad in range(4):
             nc.sync.dma_start(key_scales[32 * quad : 32 * quad + 4, :], picked_scales[SCALE_ROW0 + 4 * quad : SCALE_ROW0 + 4 * quad + 4, :])
@@ -74,11 +74,11 @@ def tile_attend_soft_topk_kernel(tc, qT, k_words, k_scales, vT, vs, offs, out):
         vs_row = shared.tile([P, P, PACK], F32, name="vs_row", offset=5 * pool_bytes)
         nc.scalar.activation(vs_row[:].rearrange("r p t -> r (p t)"), vs_pool[:].indirect(offsets[:]), ACT.Copy)
 
-        q_codes = sb.tile([P, NQ], U32, name="q_codes", align_bytes=64)
-        q_scales = sb.tile([P, NQ], U8, name="q_scales", align_bytes=64)
+        q_codes = sb.tile([P, NQ], U32, name="q_codes", align_bytes=256)
+        q_scales = sb.tile([P, NQ], U8, name="q_scales", align_bytes=256)
         nc.vector.quantize_mx(out=q_codes[:].bitcast(FP8X4), scales=q_scales[:], in_=q_bf[:].rearrange("p q t -> p (q t)"))
 
-        key_codes = shared.tile([P, N], U32, name="key_codes", align_bytes=64, offset=4 * pool_bytes)
+        key_codes = shared.tile([P, N], U32, name="key_codes", align_bytes=256, offset=4 * pool_bytes)
         for half in range(2):
             nc.vector.tensor_copy(key_codes[:, half * HALF : (half + 1) * HALF],
                                   key_pool[:].bitcast(U32).indirect(offsets[:, half * HALF // 16 : (half + 1) * HALF // 16]))
@@ -102,13 +102,13 @@ def tile_attend_soft_topk_kernel(tc, qT, k_words, k_scales, vT, vs, offs, out):
             return turned
 
         def group_values(h, turned):
-            grouped = shared.tile([P, P, 2], F32, name="v_grouped%d" % h, align_bytes=64, offset=2 * pool_bytes + 5120)
+            grouped = shared.tile([P, P, 2], F32, name="v_grouped%d" % h, align_bytes=256, offset=2 * pool_bytes + 5120)
             nc.scalar.copy(grouped[:], turned[:].rearrange("p u f -> p f u"))
             return grouped
 
         def quantize_values(h, grouped):
-            codes = shared.tile([P, P], U32, name="v_codes%d" % h, align_bytes=64, offset=2 * pool_bytes + 1024 + 512 * h)
-            scales = sb.tile([P, P], U8, name="v_scales%d" % h, align_bytes=64)
+            codes = shared.tile([P, P], U32, name="v_codes%d" % h, align_bytes=256, offset=2 * pool_bytes + 1024 + 512 * h)
+            scales = sb.tile([P, P], U8, name="v_scales%d" % h, align_bytes=256)
             nc.vector.quantize_mx(out=codes[:].bitcast(FP8X4), scales=scales[:],
                                   in_=grouped[:].rearrange("p f u -> p (f u)").bitcast(BF16))
             return codes, scales
@@ -116,7 +116,7 @@ def tile_attend_soft_topk_kernel(tc, qT, k_words, k_scales, vT, vs, offs, out):
         neg_max = shared.tile([P, 1], F32, name="neg_max", offset=4 * pool_bytes + 1024)
         nc.vector.tensor_reduce(neg_max[:], scores[:], mybir.AxisListType.X, ALU.max, negate=True)
 
-        pairs0 = shared.tile([P, 2, P, 2], BF16, name="v_pairs0", align_bytes=64, offset=4 * pool_bytes)
+        pairs0 = shared.tile([P, 2, P, 2], BF16, name="v_pairs0", align_bytes=256, offset=4 * pool_bytes)
         nc.vector.tensor_copy(pairs0[:].rearrange("f u p e -> f p u e"), v_pool0[:].indirect(offsets[:]))
 
         p_exp = sb.tile([P, PACK, P], F32, name="p_exp")
@@ -131,30 +131,30 @@ def tile_attend_soft_topk_kernel(tc, qT, k_words, k_scales, vT, vs, offs, out):
         nc.scalar.activation(row_sum[:], part_sums[0][:], ACT.Identity, bias=part_sums[1][:])
         grouped0 = group_values(0, turn_values(0, [pairs0[:, u].rearrange("f p e -> f (p e)").bitcast(F32) for u in range(2)]))
 
-        pairs1 = shared.tile([P, N], BF16, name="v_pairs1", align_bytes=64, offset=4 * pool_bytes + 1024)
+        pairs1 = shared.tile([P, N], BF16, name="v_pairs1", align_bytes=256, offset=4 * pool_bytes + 1024)
         nc.vector.tensor_copy(pairs1[:, :SPLIT], v_pool1[:].indirect(offsets[:, : SPLIT // 16]))
         nc.scalar.activation(pairs1[:, SPLIT:], v_pool1[:].indirect(offsets[:, SPLIT // 16 :]), ACT.Copy)
         turned1 = turn_values(1, [pairs1[:].bitcast(F32)[:, u::2] for u in range(2)])
-        grouped1 = [shared.tile([P, PART, 2], F32, name="v_grouped1_%d" % j, align_bytes=64, offset=1024 + 512 * j) for j in range(2)]
+        grouped1 = [shared.tile([P, PART, 2], F32, name="v_grouped1_%d" % j, align_bytes=256, offset=1024 + 512 * j) for j in range(2)]
         for j in range(2):
             nc.scalar.copy(grouped1[j][:], turned1[:, :, j * PART : (j + 1) * PART].rearrange("p u f -> p f u"))
 
-        w_bf = shared.tile([P, NQ, PACK], BF16, name="w_bf", align_bytes=64, offset=2 * pool_bytes + 4096)
+        w_bf = shared.tile([P, NQ, PACK], BF16, name="w_bf", align_bytes=256, offset=2 * pool_bytes + 4096)
         nc.vector.tensor_tensor(w_bf[:], p_turned[:].rearrange("p t q -> p q t"), vs_slot[:].to_broadcast([P, NQ, PACK]), ALU.mult)
         v0_codes, v0_scales = quantize_values(0, grouped0)
-        w_codes = shared.tile([P, NQ], U32, name="w_codes", align_bytes=64, offset=2 * pool_bytes)
-        w_scales = sb.tile([P, NQ], U8, name="w_scales", align_bytes=64)
+        w_codes = shared.tile([P, NQ], U32, name="w_codes", align_bytes=256, offset=2 * pool_bytes)
+        w_scales = sb.tile([P, NQ], U8, name="w_scales", align_bytes=256)
         nc.vector.quantize_mx(out=w_codes[:].bitcast(FP8X4), scales=w_scales[:], in_=w_bf[:].rearrange("p q t -> p (q t)"))
         inv_sum = shared.tile([P, 1], F32, name="inv_sum", offset=pool_bytes)
         nc.vector.reciprocal(inv_sum[:], row_sum[:])
-        v1_codes = shared.tile([P, P], U32, name="v_codes1", align_bytes=64, offset=2 * pool_bytes + 1024 + 512)
-        v1_scales = sb.tile([P, P], U8, name="v_scales1", align_bytes=64)
+        v1_codes = shared.tile([P, P], U32, name="v_codes1", align_bytes=256, offset=2 * pool_bytes + 1024 + 512)
+        v1_scales = sb.tile([P, P], U8, name="v_scales1", align_bytes=256)
         for j in range(2):
             cols = slice(j * PART, (j + 1) * PART)
             nc.vector.quantize_mx(out=v1_codes[:, cols].bitcast(FP8X4), scales=v1_scales[:, cols],
                                   in_=grouped1[j][:].rearrange("p f u -> p (f u)").bitcast(BF16))
 
-        y = sb.tile([NQ, DV], F32, name="y")
+        y = sb.tile([NQ, DV], F32, name="y", align_bytes=256)
         parts = ((v0_codes[:], v0_scales[:], 0, P), (v1_codes[:, :PART], v1_scales[:, :PART], P, PART),
                  (v1_codes[:, PART:], v1_scales[:, PART:], P + PART, PART))
         for h, (codes, scales, first, width) in enumerate(parts):

@@ -116,8 +116,8 @@ def tile_attend_soft_topk_kernel(tc, qT, k_words, k_scales, vT, vs, offs, out):
         neg_max = shared.tile([P, 1], F32, name="neg_max", offset=4 * pool_bytes + 1024)
         nc.vector.tensor_reduce(neg_max[:], scores[:], mybir.AxisListType.X, ALU.max, negate=True)
 
-        pairs0 = shared.tile([P, 2, P, 2], BF16, name="v_pairs0", align_bytes=256, offset=4 * pool_bytes)
-        nc.vector.tensor_copy(pairs0[:].rearrange("f u p e -> f p u e"), v_pool0[:].indirect(offsets[:]))
+        pairs0 = shared.tile([P, N], BF16, name="v_pairs0", align_bytes=256, offset=4 * pool_bytes)
+        nc.vector.tensor_copy(pairs0[:], v_pool0[:].indirect(offsets[:]))
 
         p_exp = sb.tile([P, PACK, P], F32, name="p_exp")
         part_sums = [sb.tile([P, 1], F32, name="part_sum%d" % u) for u in range(2)]
@@ -129,7 +129,7 @@ def tile_attend_soft_topk_kernel(tc, qT, k_words, k_scales, vT, vs, offs, out):
             nc.tensor.transpose(p_turned[:, t, :], p_exp[:, t, :], ident[:])
         row_sum = sb.tile([P, 1], F32, name="row_sum")
         nc.scalar.activation(row_sum[:], part_sums[0][:], ACT.Identity, bias=part_sums[1][:])
-        grouped0 = group_values(0, turn_values(0, [pairs0[:, u].rearrange("f p e -> f (p e)").bitcast(F32) for u in range(2)]))
+        grouped0 = group_values(0, turn_values(0, [pairs0[:].bitcast(F32)[:, u::2] for u in range(2)]))
 
         pairs1 = shared.tile([P, N], BF16, name="v_pairs1", align_bytes=256, offset=4 * pool_bytes + 1024)
         nc.vector.tensor_copy(pairs1[:, :SPLIT], v_pool1[:].indirect(offsets[:, : SPLIT // 16]))

from contextlib import ExitStack

import concourse.mybir as mybir

N, T, D, DV, NQ = 512, 2048, 512, 256, 128
FLOPS = 2 * NQ * N * (D + DV)

F32 = mybir.dt.float32
BF16 = mybir.dt.bfloat16
I32 = mybir.dt.int32
U32 = mybir.dt.uint32
U16 = mybir.dt.uint16
U8 = mybir.dt.uint8
FP8X4 = mybir.dt.float8_e4m3fn_x4
ACT = mybir.ActivationFunctionType
ALU = mybir.AluOpType

P = 128
PACK = 4
VS_ROW = P - 1
SCALE_ROWS = D // 32
SCALE_ROW0 = P - SCALE_ROWS
EARLY = 960
HALF = N // 2
SPLIT = 256
PART = P // 2


def tile_attend_soft_topk_kernel(tc, qT, k_words, k_scales, vT, vs, offs, out):
    nc = tc.nc
    with ExitStack() as ctx:
        sb = ctx.enter_context(tc.tile_pool(name="sb", bufs=1))
        ps = ctx.enter_context(tc.psum_pool(name="ps", bufs=1))

        shared = ctx.enter_context(tc.tile_pool(name="shared", bufs=1))
        pool_bytes = 4 * T
        offsets = sb.tile([P, N // 16], U16, name="offsets", align_bytes=256)
        q_raw = shared.tile([P, PACK, NQ], F32, name="q_raw", offset=5 * pool_bytes)
        key_scale_pool = shared.tile([P, T // 4], I32, name="key_scale_pool", offset=2 * pool_bytes - 1024)
        vs_pool = shared.tile([P, T], F32, name="vs_pool", offset=3 * pool_bytes)

        nc.vector.memset(key_scale_pool[:SCALE_ROW0, :], 0)
        nc.vector.memset(vs_pool[:VS_ROW, :], 0.0)
        nc.scalar.dma_start(key_scale_pool[SCALE_ROW0:, :], k_scales[0].bitcast(I32))
        nc.sync.dma_start(offsets[:], offs)
        nc.scalar.dma_start(vs_pool[VS_ROW:, :], vs[0:1, :])
        nc.sync.dma_start(q_raw[:], qT[0].rearrange("(p t) q -> p t q", t=PACK))

        ident = sb.tile([P, P], F32, name="ident")
        nc.gpsimd.memset(ident[:], 0.0)
        nc.gpsimd.affine_select(out=ident[:], in_=ident[:], compare_op=ALU.not_equal, fill=1.0, base=0,
                                pattern=[[-1, P]], channel_multiplier=1)
        key_scales = sb.tile([P, N // 4], I32, name="key_scales", align_bytes=256)
        nc.vector.memset(key_scales[:], 0)

        key_pool = sb.tile([P, T], I32, name="key_pool", align_bytes=256)
        nc.sync.dma_start(key_pool[:], k_words[0].rearrange("p t r -> p (t r)").bitcast(I32))

        v_early = sb.tile([P, EARLY], F32, name="v_early", align_bytes=256)
        nc.sync.dma_start(v_early[:], vT[:P, :EARLY])

        q_bf = sb.tile([P, NQ, PACK], BF16, name="q_bf", align_bytes=256)
        nc.scalar.copy(q_bf[:], q_raw[:].rearrange("p t q -> p q t"))

        picked_scales = sb.tile([P, N // 4], I32, name="picked_scales", align_bytes=256)
        nc.vector.tensor_copy(picked_scales[:].bitcast(U8), key_scale_pool[:].bitcast(U8).indirect(offsets[:]))
        for quad in range(4):
            nc.sync.dma_start(key_scales[32 * quad : 32 * quad + 4, :], picked_scales[SCALE_ROW0 + 4 * quad : SCALE_ROW0 + 4 * quad + 4, :])
        v_pool0 = shared.tile([P, T], F32, name="v_pool0", offset=pool_bytes)
        nc.sync.dma_start(v_pool0[:, EARLY:], vT[:P, EARLY:])
        v_pool1 = shared.tile([P, T], F32, name="v_pool1", offset=2 * pool_bytes)
        nc.sync.dma_start(v_pool1[:], vT[P:, :])

        vs_row = shared.tile([P, P, PACK], F32, name="vs_row", offset=5 * pool_bytes)
        nc.scalar.activation(vs_row[:].rearrange("r p t -> r (p t)"), vs_pool[:].indirect(offsets[:]), ACT.Copy)

        q_codes = sb.tile([P, NQ], U32, name="q_codes", align_bytes=256)
        q_scales = sb.tile([P, NQ], U8, name="q_scales", align_bytes=256)
        nc.vector.quantize_mx(out=q_codes[:].bitcast(FP8X4), scales=q_scales[:], in_=q_bf[:].rearrange("p q t -> p (q t)"))

        key_codes = shared.tile([P, N], U32, name="key_codes", align_bytes=256, offset=4 * pool_bytes)
        for half in range(2):
            nc.vector.tensor_copy(key_codes[:, half * HALF : (half + 1) * HALF],
                                  key_pool[:].bitcast(U32).indirect(offsets[:, half * HALF // 16 : (half + 1) * HALF // 16]))

        vs_turned = ps.tile([P, PACK, P], F32, name="vs_turned")
        for t in range(PACK):
            nc.tensor.transpose(vs_turned[:, t, :], vs_row[:, :, t], ident[:])
        vs_slot = sb.tile([P, 1, PACK], F32, name="vs_slot")
        nc.scalar.copy(vs_slot[:, 0, :], vs_turned[:, :, VS_ROW])
        nc.scalar.copy(v_pool0[:, :EARLY], v_early[:])
        scores = ps.tile([P, N], F32, name="scores", tag="turned0")
        for half in range(2):
            cols = slice(half * HALF, (half + 1) * HALF)
            nc.tensor.matmul_mx(out=scores[:, cols], lhsT=q_codes[:].bitcast(FP8X4), lhsT_scale=q_scales[:],
                                rhs=key_codes[:, cols].bitcast(FP8X4), rhs_scale=key_scales[:].bitcast(U8)[:, cols], start=True, stop=True)

        def turn_values(h, halves):
            turned = ps.tile([P, 2, P], F32, name="v_turned%d" % h, tag="turned%d" % h)
            for u in range(2):
                nc.tensor.transpose(turned[:, u, :], halves[u], ident[:])
            return turned

        def group_values(h, turned):
            grouped = shared.tile([P, P, 2], F32, name="v_grouped%d" % h, align_bytes=256, offset=2 * pool_bytes + 5120)
            nc.scalar.copy(grouped[:], turned[:].rearrange("p u f -> p f u"))
            return grouped

        def quantize_values(h, grouped):
            codes = shared.tile([P, P], U32, name="v_codes%d" % h, align_bytes=256, offset=2 * pool_bytes + 1024 + 512 * h)
            scales = sb.tile([P, P], U8, name="v_scales%d" % h, align_bytes=256)
            nc.vector.quantize_mx(out=codes[:].bitcast(FP8X4), scales=scales[:],
                                  in_=grouped[:].rearrange("p f u -> p (f u)").bitcast(BF16))
            return codes, scales

        neg_max = shared.tile([P, 1], F32, name="neg_max", offset=4 * pool_bytes + 1024)
        nc.vector.tensor_reduce(neg_max[:], scores[:], mybir.AxisListType.X, ALU.max, negate=True)

        pairs0 = shared.tile([P, N], BF16, name="v_pairs0", align_bytes=256, offset=4 * pool_bytes)
        nc.vector.tensor_copy(pairs0[:], v_pool0[:].indirect(offsets[:]))

        p_exp = sb.tile([P, PACK, P], F32, name="p_exp")
        part_sums = [sb.tile([P, 1], F32, name="part_sum%d" % u) for u in range(2)]
        by_place = scores[:].rearrange("q (p t) -> q t p", t=PACK)
        for u in range(2):
            nc.scalar.activation(p_exp[:, 2 * u : 2 * u + 2, :], by_place[:, 2 * u : 2 * u + 2, :], ACT.Exp, bias=neg_max[:], accum_out=part_sums[u][:])
        p_turned = ps.tile([P, PACK, NQ], F32, name="p_turned")
        for t in range(PACK):
            nc.tensor.transpose(p_turned[:, t, :], p_exp[:, t, :], ident[:])
        row_sum = sb.tile([P, 1], F32, name="row_sum")
        nc.scalar.activation(row_sum[:], part_sums[0][:], ACT.Identity, bias=part_sums[1][:])
        grouped0 = group_values(0, turn_values(0, [pairs0[:].bitcast(F32)[:, u::2] for u in range(2)]))

        pairs1 = shared.tile([P, N], BF16, name="v_pairs1", align_bytes=256, offset=4 * pool_bytes + 1024)
        nc.vector.tensor_copy(pairs1[:, :SPLIT], v_pool1[:].indirect(offsets[:, : SPLIT // 16]))
        nc.scalar.activation(pairs1[:, SPLIT:], v_pool1[:].indirect(offsets[:, SPLIT // 16 :]), ACT.Copy)
        turned1 = turn_values(1, [pairs1[:].bitcast(F32)[:, u::2] for u in range(2)])
        grouped1 = [shared.tile([P, PART, 2], F32, name="v_grouped1_%d" % j, align_bytes=256, offset=1024 + 512 * j) for j in range(2)]
        for j in range(2):
            nc.scalar.copy(grouped1[j][:], turned1[:, :, j * PART : (j + 1) * PART].rearrange("p u f -> p f u"))

        w_bf = shared.tile([P, NQ, PACK], BF16, name="w_bf", align_bytes=256, offset=2 * pool_bytes + 4096)
        nc.vector.tensor_tensor(w_bf[:], p_turned[:].rearrange("p t q -> p q t"), vs_slot[:].to_broadcast([P, NQ, PACK]), ALU.mult)
        v0_codes, v0_scales = quantize_values(0, grouped0)
        w_codes = shared.tile([P, NQ], U32, name="w_codes", align_bytes=256, offset=2 * pool_bytes)
        w_scales = sb.tile([P, NQ], U8, name="w_scales", align_bytes=256)
        nc.vector.quantize_mx(out=w_codes[:].bitcast(FP8X4), scales=w_scales[:], in_=w_bf[:].rearrange("p q t -> p (q t)"))
        inv_sum = shared.tile([P, 1], F32, name="inv_sum", offset=pool_bytes)
        nc.vector.reciprocal(inv_sum[:], row_sum[:])
        v1_codes = shared.tile([P, P], U32, name="v_codes1", align_bytes=256, offset=2 * pool_bytes + 1024 + 512)
        v1_scales = sb.tile([P, P], U8, name="v_scales1", align_bytes=256)
        for j in range(2):
            cols = slice(j * PART, (j + 1) * PART)
            nc.vector.quantize_mx(out=v1_codes[:, cols].bitcast(FP8X4), scales=v1_scales[:, cols],
                                  in_=grouped1[j][:].rearrange("p f u -> p (f u)").bitcast(BF16))

        y = sb.tile([NQ, DV], F32, name="y", align_bytes=256)
        parts = ((v0_codes[:], v0_scales[:], 0, P), (v1_codes[:, :PART], v1_scales[:, :PART], P, PART),
                 (v1_codes[:, PART:], v1_scales[:, PART:], P + PART, PART))
        for h, (codes, scales, first, width) in enumerate(parts):
            acc = ps.tile([NQ, width], F32, name="acc%d" % h)
            nc.tensor.matmul_mx(out=acc[:], lhsT=w_codes[:].bitcast(FP8X4), lhsT_scale=w_scales[:],
                                rhs=codes.bitcast(FP8X4), rhs_scale=scales, start=True, stop=True)
            if h == 0:
                nc.scalar.activation(y[:, first : first + width], acc[:], ACT.Copy, scale=inv_sum[:])
            else:
                nc.vector.tensor_scalar(y[:, first : first + width], acc[:], inv_sum[:], None, ALU.mult)
        nc.sync.dma_start(out[0][:, :P], y[:, :P])
        nc.sync.dma_start(out[0][:, P:], y[:, P:])
